import numpy as np
import ml_dtypes


def mxq(x, axis, fmt="e4m3"):
    dtype, down = {"e4m3": (ml_dtypes.float8_e4m3fn, 7), "e5m2": (ml_dtypes.float8_e5m2, 14)}[fmt]
    v = np.moveaxis(np.asarray(x, np.float32).astype(ml_dtypes.bfloat16).astype(np.float64), axis, -1)
    blocks = v.reshape(v.shape[:-1] + (-1, 32))
    amax = np.abs(blocks).max(-1, keepdims=True)
    byte = np.maximum(np.where(amax > 0, np.frexp(amax)[1] - 1 + 127, 0) - down, 1)
    scale = np.exp2(byte - 127.0)
    codes = (blocks / scale).astype(np.float32).astype(dtype).astype(np.float64)
    return np.moveaxis((codes * scale).reshape(v.shape), -1, axis)


WIDE = False


def mx_kscale(k):
    if not WIDE:
        return np.ones(k)
    levels = np.array([18, -18])
    if k % 512:
        return np.exp2(np.random.permutation(np.resize(levels, k // 32))).repeat(32)
    a = np.empty((k // 512, 16))
    for p in range(k // 512):
        a[p, :8] = np.random.permutation(np.resize(levels, 8))
        for g in range(8):
            far = levels[np.abs(levels - a[p, g]) >= 10]
            a[p, g + 8] = far[np.random.randint(len(far))]
    return np.exp2(a.ravel()).repeat(32)


def f64(x):
    return np.asarray(x).astype(np.float64)


def striped(idx):
    return np.tile(np.asarray(idx).reshape(-1, 16).T, (8, 1)).astype(np.uint16)


def unstriped(offs):
    return offs[:16].T.reshape(-1).astype(np.int64)


E2M1 = np.array([0.0, 0.5, 1.0, 1.5, 2.0, 3.0, 4.0, 6.0, -0.0, -0.5, -1.0, -1.5, -2.0, -3.0, -4.0, -6.0])


def pack_weight(w, fmt):
    k, n = w.shape
    w = f64(np.asarray(w, np.float32).astype(ml_dtypes.bfloat16)).reshape(k // 32, 32, n)
    amax = np.abs(w).max(1)
    if fmt == "e4m3":
        byte = np.frexp(amax)[1] - 1 + 127 - 7
    else:
        mant, ex = np.frexp(amax / 6.0)
        byte = np.where(mant > 0.5, ex, ex - 1) + 127
    byte = np.clip(np.where(amax > 0, byte, 1), 1, 254)
    scaled = (w * np.exp2(127.0 - byte)[:, None, :]).reshape(k, n).astype(np.float32)
    by_word = np.ascontiguousarray(scaled.reshape(k // 512, 128, 4, n).transpose(0, 1, 3, 2))
    if fmt == "e4m3":
        words = by_word.astype(ml_dtypes.float8_e4m3fn).view(np.uint8)
    else:
        c = by_word.astype(ml_dtypes.float4_e2m1fn).view(np.uint8) & 0xF
        words = (c[..., 0::2] | (c[..., 1::2] << 4)).reshape(k // 512, 128, 2 * n)
    return np.ascontiguousarray(words), np.ascontiguousarray(byte.astype(np.uint8).reshape(k // 512, 16, n))


def unpack_weight(words, scales, fmt):
    g, _, n = scales.shape
    words = np.ascontiguousarray(words).reshape(g, 128, n, -1)
    if fmt == "e4m3":
        vals = words.view(ml_dtypes.float8_e4m3fn).astype(np.float64)
    else:
        nib = np.empty((g, 128, n, 4), np.uint8)
        nib[..., 0::2] = words & 0xF
        nib[..., 1::2] = words >> 4
        vals = E2M1[nib]
    vals = vals * np.repeat(np.exp2(scales.astype(np.float64) - 127.0), 8, axis=1)[..., None]
    return vals.transpose(0, 1, 3, 2).reshape(g * 512, n)


def setup_inputs():
    n = np.random.standard_normal
    uni = np.random.uniform
    idx = np.random.permutation(2048)[:512]
    f_d = mx_kscale(512)
    wo_ = pack_weight(n((512, 512)) / np.sqrt(512) / f_d[:, None], "e4m3")
    return {
        "dyT": (n((512, 2048)) * f_d[:, None]).astype(np.float32),
        "oT": (n((512, 2048))).astype(np.float32),
        "wo_words": wo_[0],
        "wo_scales": wo_[1],
        "gq": np.tile(uni(0.75, 1.3, 2048), (128, 1)).astype(np.float32),
        "offs": striped(idx),
    }


def reference(dyT, oT, wo_words, wo_scales, gq, offs):
    idx = unstriped(offs)
    dyT_i = f64(dyT)[:, idx]
    o_ = f64(oT)[:, idx]
    wo = unpack_weight(wo_words, wo_scales, "e4m3")
    gq_i = f64(gq)[:1][:, idx]
    b = wo.T @ mxq(dyT_i, 0, "e5m2")
    do = gq_i * b
    q = do * o_
    qt = q.T
    dl = (qt).sum(-1, keepdims=True)
    out_0 = np.zeros((512, 2048))
    out_0[:, idx] = do
    out_1 = dl.T
    return out_0, out_1

@@ -1,0 +1,169 @@
+from contextlib import ExitStack
+
+import concourse.mybir as mybir
+from concourse.masks import make_identity
+
+D, E, SLOTS, T = 512, 512, 512, 2048
+P = 128
+PACK = 4
+TILES = E // P
+BLOCKS = SLOTS // P
+BANK = 512
+QUAD = 32
+PER_COLUMN = 16
+
+FLOPS = 2 * D * E * SLOTS
+BYTES = 4 * (D * T + 2 * E * T + T + SLOTS) + D * E + D * E // 32 + 2 * P * SLOTS // 16
+
+F32 = mybir.dt.float32
+BF16 = mybir.dt.bfloat16
+I32 = mybir.dt.int32
+U32 = mybir.dt.uint32
+U16 = mybir.dt.uint16
+U8 = mybir.dt.uint8
+E4M3 = mybir.dt.float8_e4m3fn_x4
+E5M2 = mybir.dt.float8_e5m2_x4
+MULT = mybir.AluOpType.mult
+ADD = mybir.AluOpType.add
+COPY = mybir.ActivationFunctionType.Copy
+
+
+def tile_attend_gdelta_kernel(tc, dyT, oT, wo_words, wo_scales, gq, offs, out_0, out_1):
+    nc = tc.nc
+    with ExitStack() as ctx:
+        keep = ctx.enter_context(tc.tile_pool(name="keep", bufs=1))
+        psum = ctx.enter_context(tc.psum_pool(name="psum", bufs=1))
+
+        offsets = keep.tile([P, SLOTS // PER_COLUMN], U16, name="offsets")
+        nc.sync.dma_start(offsets[:], offs)
+
+        dy_planes = [keep.tile([P, T], F32, name="dy%d" % t) for t in range(PACK)]
+        dy_rows = dyT.rearrange("(p t) w -> t p w", t=PACK)
+        for t in range(PACK):
+            nc.sync.dma_start(out=dy_planes[t][:], in_=dy_rows[t])
+
+        gate_rows = keep.tile([P, P], F32, name="gate_rows")
+        nc.scalar.dma_start(out=gate_rows[:], in_=gq[0 : P * P // T, :].rearrange("r (c p) -> (r c) p", p=P))
+
+        w_scales = keep.tile([P, E], U8, name="w_scales", align_bytes=64)
+        nc.vector.memset(w_scales[:].bitcast(I32), 0)
+        for quad in range(P // QUAD):
+            nc.scalar.dma_start(
+                out=w_scales[QUAD * quad : QUAD * quad + 4, :].bitcast(I32),
+                in_=wo_scales[0, 4 * quad : 4 * quad + 4, :].bitcast(I32),
+            )
+
+        w_words = keep.tile([P, E], U32, name="w_words", align_bytes=64)
+        nc.sync.dma_start(
+            out=w_words[:].bitcast(I32), in_=wo_words[0].rearrange("p n t -> p (n t)").bitcast(I32)
+        )
+
+        o_tiles = [keep.tile([P, T], F32, name="o%d" % m) for m in range(TILES)]
+        for m in range(TILES):
+            nc.sync.dma_start(out=o_tiles[m][:], in_=oT[m * P : (m + 1) * P, :])
+
+        ident = keep.tile([P, P], F32, name="ident")
+        make_identity(nc, ident[:])
+        delta_cols = keep.tile([P, P], F32, name="delta_cols", align_bytes=64)
+        nc.gpsimd.memset(delta_cols[:], 0.0)
+
+        windows = [keep.tile([P, T], F32, name="window%d" % m) for m in range(TILES)]
+        for m in range(TILES):
+            nc.vector.memset(windows[m][:], 0.0)
+
+        turned = psum.tile([P, P], F32, name="turned", tag="sum0")
+        nc.tensor.transpose(turned[:], gate_rows[:], ident[:])
+        gate_turned = keep.tile([P, T // P], F32, name="gate_turned")
+        nc.scalar.copy(out=gate_turned[:], in_=turned[:, 0 : T // P])
+        gate_table = keep.tile([P, T], F32, name="gate_table")
+        for b in range(T // BANK):
+            spread = psum.tile([P, BANK], F32, name="spread", tag="prod%d" % b)
+            for c in range(BANK // P):
+                col = b * (BANK // P) + c
+                nc.tensor.transpose(
+                    spread[:, c * P : (c + 1) * P], gate_turned[:, col : col + 1].to_broadcast([P, P]), ident[:]
+                )
+            nc.scalar.copy(out=gate_table[:, b * BANK : (b + 1) * BANK], in_=spread[:])
+
+        grouped = keep.tile([P, SLOTS, PACK], BF16, name="grouped", align_bytes=64)
+        gate = keep.tile([P, SLOTS], F32, name="gate")
+        for t in range(PACK):
+            nc.vector.tensor_copy(grouped[:, :, t], dy_planes[t][:].indirect(offsets[:]))
+            if t == 1:
+                nc.vector.tensor_copy(gate[:], gate_table[:].indirect(offsets[:]))
+
+        gate_back = psum.tile([P, BLOCKS, P], F32, name="gate_back", tag="sum1")
+        for j in range(BLOCKS):
+            nc.tensor.transpose(gate_back[:, j, :], gate[:, j * P : (j + 1) * P], ident[:])
+        gate_cols = keep.tile([P, BLOCKS], F32, name="gate_cols")
+        nc.scalar.copy(out=gate_cols[:], in_=gate_back[:, :, 0])
+
+        dy_words = keep.tile([P, SLOTS], U32, name="dy_words", align_bytes=64)
+        dy_scales = keep.tile([P, SLOTS], U8, name="dy_scales", align_bytes=64)
+        nc.vector.quantize_mx(
+            out=dy_words[:].bitcast(E5M2), scales=dy_scales[:], in_=grouped[:].rearrange("p s t -> p (s t)")
+        )
+
+        o_first = keep.tile([P, SLOTS], F32, name="o_first")
+        nc.vector.tensor_copy(o_first[:], o_tiles[0][:].indirect(offsets[:]))
+
+        back = [keep.tile([P, SLOTS], F32, name="back%d" % m) for m in range(TILES)]
+        for m in range(TILES):
+            cols = slice(m * P, (m + 1) * P)
+            prod = psum.tile([P, SLOTS], F32, name="prod", tag="prod%d" % m)
+            nc.tensor.matmul_mx(
+                out=prod[:],
+                lhsT=w_words[:, cols].bitcast(E4M3),
+                lhsT_scale=w_scales[:, cols],
+                rhs=dy_words[:].bitcast(E5M2),
+                rhs_scale=dy_scales[:],
+                start=True,
+                stop=True,
+            )
+            nc.scalar.copy(out=back[m][:], in_=prod[:])
+
+        for m in range(TILES):
+            nc.vector.tensor_tensor(windows[m][:].indirect(offsets[:]), back[m][:], gate[:], MULT)
+            nc.sync.dma_start(out=out_0[m * P : (m + 1) * P, :], in_=windows[m][:])
+
+        sums = [psum.tile([P, P], F32, name="sum%d" % j, tag="sum%d" % j) for j in range(BLOCKS)]
+        last = SLOTS - P
+        for m in range(TILES):
+            terms = keep.tile([P, SLOTS], F32, name="terms%d" % m)
+            if m == 0:
+                nc.vector.tensor_tensor(terms[:], o_first[:], back[0][:], MULT)
+            elif m < TILES - 1:
+                nc.vector.tensor_tensor(terms[:], o_tiles[m][:].indirect(offsets[:]), back[m][:], MULT)
+            else:
+                for lo, hi in ((0, last), (last, SLOTS)):
+                    nc.vector.tensor_tensor(
+                        terms[:, lo:hi],
+                        o_tiles[m][:].indirect(offsets[:, lo // PER_COLUMN : hi // PER_COLUMN]),
+                        back[m][:, lo:hi],
+                        MULT,
+                    )
+            for j in range(BLOCKS):
+                nc.tensor.matmul(
+                    sums[j][:],
+                    lhsT=terms[:, j * P : (j + 1) * P],
+                    rhs=ident[:],
+                    is_transpose=True,
+                    start=(m == 0),
+                    stop=(m == TILES - 1),
+                )
+
+        gated = keep.tile([P, BLOCKS, P], F32, name="gated")
+        for j in range(BLOCKS):
+            delta_j = delta_cols[:, QUAD * j : QUAD * j + 1]
+            if j < BLOCKS - 1:
+                nc.scalar.activation(gated[:, j, :], sums[j][:], COPY, scale=gate_cols[:, j : j + 1], accum_out=delta_j)
+            else:
+                nc.vector.tensor_scalar(
+                    gated[:, j, :], sums[j][:], gate_cols[:, j : j + 1], None, MULT, ADD, accum_out=delta_j
+                )
+        delta_rows = keep.tile([P, P], F32, name="delta_rows", align_bytes=64)
+        nc.vector.transpose(delta_rows[:], delta_cols[:])
+        nc.sync.dma_start(
+            out=out_1[0].rearrange("(j q r) -> q j r", j=BLOCKS, r=QUAD),
+            in_=delta_rows[0:P:QUAD, :].rearrange("q (j r) -> q j r", r=QUAD),
+        )

@@ -11,6 +11,7 @@ BLOCKS = SLOTS // P
 BANK = 512
 QUAD = 32
 PER_COLUMN = 16
+WINDOWS = 3
 
 FLOPS = 2 * D * E * SLOTS
 BYTES = 4 * (D * T + 2 * E * T + T + SLOTS) + D * E + D * E // 32 + 2 * P * SLOTS // 16
@@ -42,21 +43,22 @@ def tile_attend_gdelta_kernel(tc, dyT, oT, wo_words, wo_scales, gq, offs, out_0,
         for t in range(PACK):
             nc.sync.dma_start(out=dy_planes[t][:], in_=dy_rows[t])
 
-        gate_rows = keep.tile([P, P], F32, name="gate_rows")
-        nc.scalar.dma_start(out=gate_rows[:], in_=gq[0 : P * P // T, :].rearrange("r (c p) -> (r c) p", p=P))
-
-        w_scales = keep.tile([P, E], U8, name="w_scales", align_bytes=64)
-        nc.vector.memset(w_scales[:].bitcast(I32), 0)
-        for quad in range(P // QUAD):
-            nc.scalar.dma_start(
-                out=w_scales[QUAD * quad : QUAD * quad + 4, :].bitcast(I32),
-                in_=wo_scales[0, 4 * quad : 4 * quad + 4, :].bitcast(I32),
-            )
+        gate_table = keep.tile([P, T], F32, name="gate_table")
+        nc.vector.memset(gate_table[:].bitcast(I32), 0)
+        nc.scalar.dma_start(out=gate_table[0:1, :], in_=gq[0:1, :])
 
         w_words = keep.tile([P, E], U32, name="w_words", align_bytes=64)
         nc.sync.dma_start(
             out=w_words[:].bitcast(I32), in_=wo_words[0].rearrange("p n t -> p (n t)").bitcast(I32)
         )
+
+        w_scales = keep.tile([P, E], U8, name="w_scales", align_bytes=64)
+        nc.gpsimd.memset(w_scales[:].bitcast(I32), 0)
+        for quad in range(P // QUAD):
+            nc.sync.dma_start(
+                out=w_scales[QUAD * quad : QUAD * quad + 4, :].bitcast(I32),
+                in_=wo_scales[0, 4 * quad : 4 * quad + 4, :].bitcast(I32),
+            )
 
         o_tiles = [keep.tile([P, T], F32, name="o%d" % m) for m in range(TILES)]
         for m in range(TILES):
@@ -67,36 +69,31 @@ def tile_attend_gdelta_kernel(tc, dyT, oT, wo_words, wo_scales, gq, offs, out_0,
         delta_cols = keep.tile([P, P], F32, name="delta_cols", align_bytes=64)
         nc.gpsimd.memset(delta_cols[:], 0.0)
 
-        windows = [keep.tile([P, T], F32, name="window%d" % m) for m in range(TILES)]
-        for m in range(TILES):
-            nc.vector.memset(windows[m][:], 0.0)
-
-        turned = psum.tile([P, P], F32, name="turned", tag="sum0")
-        nc.tensor.transpose(turned[:], gate_rows[:], ident[:])
-        gate_turned = keep.tile([P, T // P], F32, name="gate_turned")
-        nc.scalar.copy(out=gate_turned[:], in_=turned[:, 0 : T // P])
-        gate_table = keep.tile([P, T], F32, name="gate_table")
-        for b in range(T // BANK):
-            spread = psum.tile([P, BANK], F32, name="spread", tag="prod%d" % b)
-            for c in range(BANK // P):
-                col = b * (BANK // P) + c
-                nc.tensor.transpose(
-                    spread[:, c * P : (c + 1) * P], gate_turned[:, col : col + 1].to_broadcast([P, P]), ident[:]
-                )
-            nc.scalar.copy(out=gate_table[:, b * BANK : (b + 1) * BANK], in_=spread[:])
+        windows = [keep.tile([P, T], F32, name="window%d" % w) for w in range(WINDOWS)]
+        for w in range(WINDOWS):
+            nc.vector.memset(windows[w][:].bitcast(I32), 0)
 
         grouped = keep.tile([P, SLOTS, PACK], BF16, name="grouped", align_bytes=64)
-        gate = keep.tile([P, SLOTS], F32, name="gate")
-        for t in range(PACK):
-            nc.vector.tensor_copy(grouped[:, :, t], dy_planes[t][:].indirect(offsets[:]))
-            if t == 1:
-                nc.vector.tensor_copy(gate[:], gate_table[:].indirect(offsets[:]))
+        first_pair = keep.tile([P, 2, SLOTS], BF16, name="first_pair")
+        for t in range(2):
+            nc.vector.tensor_copy(first_pair[:, t, :], dy_planes[t][:].indirect(offsets[:]))
+        nc.scalar.copy(out=grouped[:, :, 0:2], in_=first_pair[:].rearrange("p t s -> p s t"))
 
-        gate_back = psum.tile([P, BLOCKS, P], F32, name="gate_back", tag="sum1")
+        gate_row = keep.tile([P, SLOTS], F32, name="gate_row")
+        nc.vector.tensor_copy(gate_row[:], gate_table[:].indirect(offsets[:]))
+        gate_turned = psum.tile([P, BLOCKS, P], F32, name="gate_turned", tag="sum0")
         for j in range(BLOCKS):
-            nc.tensor.transpose(gate_back[:, j, :], gate[:, j * P : (j + 1) * P], ident[:])
+            nc.tensor.transpose(gate_turned[:, j, :], gate_row[:, j * P : (j + 1) * P], ident[:])
         gate_cols = keep.tile([P, BLOCKS], F32, name="gate_cols")
-        nc.scalar.copy(out=gate_cols[:], in_=gate_back[:, :, 0])
+        nc.scalar.copy(out=gate_cols[:], in_=gate_turned[:, :, 0])
+        gate_spread = psum.tile([P, BLOCKS, P], F32, name="gate_spread", tag="sum1")
+        for j in range(BLOCKS):
+            nc.tensor.transpose(gate_spread[:, j, :], gate_cols[:, j : j + 1].to_broadcast([P, P]), ident[:])
+        gate = keep.tile([P, SLOTS], F32, name="gate")
+        nc.scalar.copy(out=gate[:], in_=gate_spread[:].rearrange("p j s -> p (j s)"))
+
+        for t in range(2, PACK):
+            nc.vector.tensor_copy(grouped[:, :, t], dy_planes[t][:].indirect(offsets[:]))
 
         dy_words = keep.tile([P, SLOTS], U32, name="dy_words", align_bytes=64)
         dy_scales = keep.tile([P, SLOTS], U8, name="dy_scales", align_bytes=64)
@@ -104,10 +101,12 @@ def tile_attend_gdelta_kernel(tc, dyT, oT, wo_words, wo_scales, gq, offs, out_0,
             out=dy_words[:].bitcast(E5M2), scales=dy_scales[:], in_=grouped[:].rearrange("p s t -> p (s t)")
         )
 
-        o_first = keep.tile([P, SLOTS], F32, name="o_first")
-        nc.vector.tensor_copy(o_first[:], o_tiles[0][:].indirect(offsets[:]))
+        last = SLOTS - P
+        picked = [keep.tile([P, SLOTS], F32, name="picked%d" % m) for m in range(TILES)]
+        nc.vector.tensor_copy(picked[0][:], o_tiles[0][:].indirect(offsets[:]))
 
         back = [keep.tile([P, SLOTS], F32, name="back%d" % m) for m in range(TILES)]
+        grads = [keep.tile([P, SLOTS], F32, name="grad%d" % m, tag="grad%d" % m) for m in range(TILES)]
         for m in range(TILES):
             cols = slice(m * P, (m + 1) * P)
             prod = psum.tile([P, SLOTS], F32, name="prod", tag="prod%d" % m)
@@ -120,36 +119,37 @@ def tile_attend_gdelta_kernel(tc, dyT, oT, wo_words, wo_scales, gq, offs, out_0,
                 start=True,
                 stop=True,
             )
+            if m == 0:
+                nc.vector.tensor_tensor(grads[m][:], prod[:], gate[:], MULT)
             nc.scalar.copy(out=back[m][:], in_=prod[:])
+            if m > 0:
+                nc.gpsimd.tensor_tensor(grads[m][:], back[m][:], gate[:], MULT)
 
         for m in range(TILES):
-            nc.vector.tensor_tensor(windows[m][:].indirect(offsets[:]), back[m][:], gate[:], MULT)
-            nc.sync.dma_start(out=out_0[m * P : (m + 1) * P, :], in_=windows[m][:])
+            window = windows[m % WINDOWS]
+            if m > 0:
+                width = SLOTS if m < TILES - 1 else last
+                nc.vector.tensor_copy(
+                    picked[m][:, 0:width], o_tiles[m][:].indirect(offsets[:, 0 : width // PER_COLUMN])
+                )
+            nc.vector.tensor_copy(window[:].indirect(offsets[:]), grads[m][:])
+            nc.sync.dma_start(out=out_0[m * P : (m + 1) * P, :], in_=window[:])
 
         sums = [psum.tile([P, P], F32, name="sum%d" % j, tag="sum%d" % j) for j in range(BLOCKS)]
-        last = SLOTS - P
         for m in range(TILES):
             terms = keep.tile([P, SLOTS], F32, name="terms%d" % m)
-            if m == 0:
-                nc.vector.tensor_tensor(terms[:], o_first[:], back[0][:], MULT)
-            elif m < TILES - 1:
-                nc.vector.tensor_tensor(terms[:], o_tiles[m][:].indirect(offsets[:]), back[m][:], MULT)
-            else:
-                for lo, hi in ((0, last), (last, SLOTS)):
-                    nc.vector.tensor_tensor(
-                        terms[:, lo:hi],
-                        o_tiles[m][:].indirect(offsets[:, lo // PER_COLUMN : hi // PER_COLUMN]),
-                        back[m][:, lo:hi],
-                        MULT,
-                    )
+            width = SLOTS if m < TILES - 1 else last
+            nc.gpsimd.tensor_tensor(terms[:, 0:width], picked[m][:, 0:width], back[m][:, 0:width], MULT)
+            blocks = [terms[:, j * P : (j + 1) * P] for j in range(width // P)]
+            if m == TILES - 1:
+                tail = keep.tile([P, P], F32, name="tail", tag="grad%d" % m)
+                nc.vector.tensor_tensor(
+                    tail[:], o_tiles[m][:].indirect(offsets[:, last // PER_COLUMN :]), back[m][:, last:], MULT
+                )
+                blocks.append(tail[:])
             for j in range(BLOCKS):
                 nc.tensor.matmul(
-                    sums[j][:],
-                    lhsT=terms[:, j * P : (j + 1) * P],
-                    rhs=ident[:],
-                    is_transpose=True,
-                    start=(m == 0),
-                    stop=(m == TILES - 1),
+                    sums[j][:], lhsT=blocks[j], rhs=ident[:], is_transpose=True, start=(m == 0), stop=(m == TILES - 1)
                 )
 
         gated = keep.tile([P, BLOCKS, P], F32, name="gated")

@@ -38,14 +38,13 @@ def tile_attend_gdelta_kernel(tc, dyT, oT, wo_words, wo_scales, gq, offs, out_0,
         offsets = keep.tile([P, SLOTS // PER_COLUMN], U16, name="offsets")
         nc.sync.dma_start(offsets[:], offs)
 
+        gate_line = keep.tile([1, T], F32, name="gate_line")
+        nc.scalar.dma_start(out=gate_line[:], in_=gq[0:1, :])
+
         dy_planes = [keep.tile([P, T], F32, name="dy%d" % t) for t in range(PACK)]
         dy_rows = dyT.rearrange("(p t) w -> t p w", t=PACK)
         for t in range(PACK):
             nc.sync.dma_start(out=dy_planes[t][:], in_=dy_rows[t])
-
-        gate_table = keep.tile([P, T], F32, name="gate_table")
-        nc.vector.memset(gate_table[:].bitcast(I32), 0)
-        nc.scalar.dma_start(out=gate_table[0:1, :], in_=gq[0:1, :])
 
         w_words = keep.tile([P, E], U32, name="w_words", align_bytes=64)
         nc.sync.dma_start(
@@ -54,15 +53,20 @@ def tile_attend_gdelta_kernel(tc, dyT, oT, wo_words, wo_scales, gq, offs, out_0,
 
         w_scales = keep.tile([P, E], U8, name="w_scales", align_bytes=64)
         nc.gpsimd.memset(w_scales[:].bitcast(I32), 0)
-        for quad in range(P // QUAD):
-            nc.sync.dma_start(
-                out=w_scales[QUAD * quad : QUAD * quad + 4, :].bitcast(I32),
-                in_=wo_scales[0, 4 * quad : 4 * quad + 4, :].bitcast(I32),
-            )
+
+        gate_table = keep.tile([P, T], F32, name="gate_table")
+        nc.gpsimd.memset(gate_table[:].bitcast(I32), 0)
+        nc.scalar.copy(out=gate_table[0:1, :], in_=gate_line[:])
 
         o_tiles = [keep.tile([P, T], F32, name="o%d" % m) for m in range(TILES)]
         for m in range(TILES):
             nc.sync.dma_start(out=o_tiles[m][:], in_=oT[m * P : (m + 1) * P, :])
+            if m == 0:
+                for quad in range(P // QUAD):
+                    nc.sync.dma_start(
+                        out=w_scales[QUAD * quad : QUAD * quad + 4, :].bitcast(I32),
+                        in_=wo_scales[0, 4 * quad : 4 * quad + 4, :].bitcast(I32),
+                    )
 
         ident = keep.tile([P, P], F32, name="ident")
         make_identity(nc, ident[:])
@@ -71,7 +75,7 @@ def tile_attend_gdelta_kernel(tc, dyT, oT, wo_words, wo_scales, gq, offs, out_0,
 
         windows = [keep.tile([P, T], F32, name="window%d" % w) for w in range(WINDOWS)]
         for w in range(WINDOWS):
-            nc.vector.memset(windows[w][:].bitcast(I32), 0)
+            nc.gpsimd.memset(windows[w][:].bitcast(I32), 0)
 
         grouped = keep.tile([P, SLOTS, PACK], BF16, name="grouped", align_bytes=64)
         first_pair = keep.tile([P, 2, SLOTS], BF16, name="first_pair")

@@ -12,6 +12,8 @@ BANK = 512
 QUAD = 32
 PER_COLUMN = 16
 WINDOWS = 3
+FUSED = 2
+HALF = SLOTS // 2
 
 FLOPS = 2 * D * E * SLOTS
 BYTES = 4 * (D * T + 2 * E * T + T + SLOTS) + D * E + D * E // 32 + 2 * P * SLOTS // 16
@@ -37,6 +39,7 @@ def tile_attend_gdelta_kernel(tc, dyT, oT, wo_words, wo_scales, gq, offs, out_0,
 
         offsets = keep.tile([P, SLOTS // PER_COLUMN], U16, name="offsets")
         nc.sync.dma_start(offsets[:], offs)
+        half_lists = [offsets[:, h * HALF // PER_COLUMN : (h + 1) * HALF // PER_COLUMN] for h in range(2)]
 
         gate_line = keep.tile([1, T], F32, name="gate_line")
         nc.scalar.dma_start(out=gate_line[:], in_=gq[0:1, :])
@@ -46,10 +49,11 @@ def tile_attend_gdelta_kernel(tc, dyT, oT, wo_words, wo_scales, gq, offs, out_0,
         for t in range(PACK):
             nc.sync.dma_start(out=dy_planes[t][:], in_=dy_rows[t])
 
-        w_words = keep.tile([P, E], U32, name="w_words", align_bytes=64)
-        nc.sync.dma_start(
-            out=w_words[:].bitcast(I32), in_=wo_words[0].rearrange("p n t -> p (n t)").bitcast(I32)
-        )
+        w_first = keep.tile([P, P], U32, name="w_first", align_bytes=64)
+        w_second = keep.tile([P, P], U32, name="w_second", align_bytes=64)
+        w_rest = keep.tile([P, E - 2 * P], U32, name="w_rest", align_bytes=64)
+        w_tiles = [w_first[:], w_second[:], w_rest[:, 0:P], w_rest[:, P:]]
+        w_dram = wo_words[0].rearrange("p n t -> p (n t)").bitcast(I32)
 
         w_scales = keep.tile([P, E], U8, name="w_scales", align_bytes=64)
         nc.gpsimd.memset(w_scales[:].bitcast(I32), 0)
@@ -59,14 +63,18 @@ def tile_attend_gdelta_kernel(tc, dyT, oT, wo_words, wo_scales, gq, offs, out_0,
         nc.scalar.copy(out=gate_table[0:1, :], in_=gate_line[:])
 
         o_tiles = [keep.tile([P, T], F32, name="o%d" % m) for m in range(TILES)]
+        for quad in range(P // QUAD):
+            nc.sync.dma_start(
+                out=w_scales[QUAD * quad : QUAD * quad + 4, :].bitcast(I32),
+                in_=wo_scales[0, 4 * quad : 4 * quad + 4, :].bitcast(I32),
+            )
         for m in range(TILES):
             nc.sync.dma_start(out=o_tiles[m][:], in_=oT[m * P : (m + 1) * P, :])
             if m == 0:
-                for quad in range(P // QUAD):
-                    nc.sync.dma_start(
-                        out=w_scales[QUAD * quad : QUAD * quad + 4, :].bitcast(I32),
-                        in_=wo_scales[0, 4 * quad : 4 * quad + 4, :].bitcast(I32),
-                    )
+                nc.sync.dma_start(out=w_first[:].bitcast(I32), in_=w_dram[:, 0:P])
+                nc.sync.dma_start(out=w_second[:].bitcast(I32), in_=w_dram[:, P : 2 * P])
+            if m == 2:
+                nc.sync.dma_start(out=w_rest[:].bitcast(I32), in_=w_dram[:, 2 * P :])
 
         ident = keep.tile([P, P], F32, name="ident")
         make_identity(nc, ident[:])
@@ -77,11 +85,14 @@ def tile_attend_gdelta_kernel(tc, dyT, oT, wo_words, wo_scales, gq, offs, out_0,
         for w in range(WINDOWS):
             nc.gpsimd.memset(windows[w][:].bitcast(I32), 0)
 
-        grouped = keep.tile([P, SLOTS, PACK], BF16, name="grouped", align_bytes=64)
+        grouped = [keep.tile([P, HALF, PACK], BF16, name="grouped%d" % h, align_bytes=64) for h in range(2)]
         first_pair = keep.tile([P, 2, SLOTS], BF16, name="first_pair")
         for t in range(2):
             nc.vector.tensor_copy(first_pair[:, t, :], dy_planes[t][:].indirect(offsets[:]))
-        nc.scalar.copy(out=grouped[:, :, 0:2], in_=first_pair[:].rearrange("p t s -> p s t"))
+        for h in range(2):
+            nc.scalar.copy(
+                out=grouped[h][:, :, 0:2], in_=first_pair[:, :, h * HALF : (h + 1) * HALF].rearrange("p t s -> p s t")
+            )
 
         gate_row = keep.tile([P, SLOTS], F32, name="gate_row")
         nc.vector.tensor_copy(gate_row[:], gate_table[:].indirect(offsets[:]))
@@ -93,62 +104,76 @@ def tile_attend_gdelta_kernel(tc, dyT, oT, wo_words, wo_scales, gq, offs, out_0,
         gate_spread = psum.tile([P, BLOCKS, P], F32, name="gate_spread", tag="sum1")
         for j in range(BLOCKS):
             nc.tensor.transpose(gate_spread[:, j, :], gate_cols[:, j : j + 1].to_broadcast([P, P]), ident[:])
-        gate = keep.tile([P, SLOTS], F32, name="gate")
+        gate = keep.tile([P, SLOTS], F32, name="gate", tag="gate")
         nc.scalar.copy(out=gate[:], in_=gate_spread[:].rearrange("p j s -> p (j s)"))
 
         for t in range(2, PACK):
-            nc.vector.tensor_copy(grouped[:, :, t], dy_planes[t][:].indirect(offsets[:]))
+            for h in range(2):
+                nc.vector.tensor_copy(grouped[h][:, :, t], dy_planes[t][:].indirect(half_lists[h]))
 
         dy_words = keep.tile([P, SLOTS], U32, name="dy_words", align_bytes=64)
         dy_scales = keep.tile([P, SLOTS], U8, name="dy_scales", align_bytes=64)
-        nc.vector.quantize_mx(
-            out=dy_words[:].bitcast(E5M2), scales=dy_scales[:], in_=grouped[:].rearrange("p s t -> p (s t)")
-        )
+        for h in range(2):
+            half = slice(h * HALF, (h + 1) * HALF)
+            nc.vector.quantize_mx(
+                out=dy_words[:, half].bitcast(E5M2),
+                scales=dy_scales[:, half],
+                in_=grouped[h][:].rearrange("p s t -> p (s t)"),
+            )
 
         last = SLOTS - P
-        picked = [keep.tile([P, SLOTS], F32, name="picked%d" % m) for m in range(TILES)]
-        nc.vector.tensor_copy(picked[0][:], o_tiles[0][:].indirect(offsets[:]))
+        picked = keep.tile([P, (TILES - 1) * SLOTS], F32, name="picked")
+        final = keep.tile([P, SLOTS + last], F32, name="final", tag="final")
+        picks = [picked[:, m * SLOTS : (m + 1) * SLOTS] for m in range(TILES - 1)] + [final[:, SLOTS:]]
+        back = keep.tile([P, TILES * SLOTS], F32, name="back")
+        slab = [slice(m * SLOTS, (m + 1) * SLOTS) for m in range(TILES)]
+        nc.vector.tensor_copy(picked[:, slab[0]], o_tiles[0][:].indirect(offsets[:]))
 
-        back = [keep.tile([P, SLOTS], F32, name="back%d" % m) for m in range(TILES)]
-        grads = [keep.tile([P, SLOTS], F32, name="grad%d" % m, tag="grad%d" % m) for m in range(TILES)]
+        grads = {m: keep.tile([P, SLOTS], F32, name="grad%d" % m)[:] for m in range(FUSED, TILES - 1)}
+        grads[TILES - 1] = final[:, 0:SLOTS]
         for m in range(TILES):
             cols = slice(m * P, (m + 1) * P)
             prod = psum.tile([P, SLOTS], F32, name="prod", tag="prod%d" % m)
             nc.tensor.matmul_mx(
                 out=prod[:],
-                lhsT=w_words[:, cols].bitcast(E4M3),
+                lhsT=w_tiles[m].bitcast(E4M3),
                 lhsT_scale=w_scales[:, cols],
                 rhs=dy_words[:].bitcast(E5M2),
                 rhs_scale=dy_scales[:],
                 start=True,
                 stop=True,
             )
-            if m == 0:
-                nc.vector.tensor_tensor(grads[m][:], prod[:], gate[:], MULT)
-            nc.scalar.copy(out=back[m][:], in_=prod[:])
-            if m > 0:
-                nc.gpsimd.tensor_tensor(grads[m][:], back[m][:], gate[:], MULT)
+            nc.scalar.copy(out=back[:, slab[m]], in_=prod[:])
+            if m >= FUSED:
+                nc.gpsimd.tensor_tensor(grads[m], back[:, slab[m]], gate[:], MULT)
 
-        for m in range(TILES):
+        for m in range(FUSED):
+            nc.vector.tensor_tensor(windows[m][:].indirect(offsets[:]), back[:, slab[m]], gate[:], MULT)
+            nc.sync.dma_start(out=out_0[m * P : (m + 1) * P, :], in_=windows[m][:])
+        for m in range(1, TILES):
+            width = SLOTS if m < TILES - 1 else last
+            nc.vector.tensor_copy(picks[m], o_tiles[m][:].indirect(offsets[:, 0 : width // PER_COLUMN]))
+        for m in range(FUSED, TILES):
             window = windows[m % WINDOWS]
-            if m > 0:
-                width = SLOTS if m < TILES - 1 else last
-                nc.vector.tensor_copy(
-                    picked[m][:, 0:width], o_tiles[m][:].indirect(offsets[:, 0 : width // PER_COLUMN])
-                )
-            nc.vector.tensor_copy(window[:].indirect(offsets[:]), grads[m][:])
+            nc.vector.tensor_copy(window[:].indirect(offsets[:]), grads[m])
             nc.sync.dma_start(out=out_0[m * P : (m + 1) * P, :], in_=window[:])
 
         sums = [psum.tile([P, P], F32, name="sum%d" % j, tag="sum%d" % j) for j in range(BLOCKS)]
+        early = keep.tile([P, FUSED * SLOTS], F32, name="early", tag="gate")
+        nc.gpsimd.tensor_tensor(early[:], picked[:, 0 : FUSED * SLOTS], back[:, 0 : FUSED * SLOTS], MULT)
         for m in range(TILES):
-            terms = keep.tile([P, SLOTS], F32, name="terms%d" % m)
             width = SLOTS if m < TILES - 1 else last
-            nc.gpsimd.tensor_tensor(terms[:, 0:width], picked[m][:, 0:width], back[m][:, 0:width], MULT)
+            if m < FUSED:
+                terms = early[:, slab[m]]
+            else:
+                terms = keep.tile([P, width], F32, name="terms%d" % m)[:]
+                cols = slice(m * SLOTS, m * SLOTS + width)
+                nc.gpsimd.tensor_tensor(terms, picks[m], back[:, cols], MULT)
             blocks = [terms[:, j * P : (j + 1) * P] for j in range(width // P)]
             if m == TILES - 1:
-                tail = keep.tile([P, P], F32, name="tail", tag="grad%d" % m)
+                tail = keep.tile([P, P], F32, name="tail", tag="final")
                 nc.vector.tensor_tensor(
-                    tail[:], o_tiles[m][:].indirect(offsets[:, last // PER_COLUMN :]), back[m][:, last:], MULT
+                    tail[:], o_tiles[m][:].indirect(offsets[:, last // PER_COLUMN :]), back[:, m * SLOTS + last :], MULT
                 )
                 blocks.append(tail[:])
             for j in range(BLOCKS):

@@ -11,8 +11,9 @@ BLOCKS = SLOTS // P
 BANK = 512
 QUAD = 32
 PER_COLUMN = 16
-WINDOWS = 3
+WINDOWS = 4
 FUSED = 2
+LATE = 2
 HALF = SLOTS // 2
 
 FLOPS = 2 * D * E * SLOTS
@@ -38,7 +39,6 @@ def tile_attend_gdelta_kernel(tc, dyT, oT, wo_words, wo_scales, gq, offs, out_0,
         psum = ctx.enter_context(tc.psum_pool(name="psum", bufs=1))
 
         offsets = keep.tile([P, SLOTS // PER_COLUMN], U16, name="offsets")
-        nc.sync.dma_start(offsets[:], offs)
         half_lists = [offsets[:, h * HALF // PER_COLUMN : (h + 1) * HALF // PER_COLUMN] for h in range(2)]
 
         gate_line = keep.tile([1, T], F32, name="gate_line")
@@ -48,6 +48,8 @@ def tile_attend_gdelta_kernel(tc, dyT, oT, wo_words, wo_scales, gq, offs, out_0,
         dy_rows = dyT.rearrange("(p t) w -> t p w", t=PACK)
         for t in range(PACK):
             nc.sync.dma_start(out=dy_planes[t][:], in_=dy_rows[t])
+            if t == 0:
+                nc.sync.dma_start(offsets[:], offs)
 
         w_first = keep.tile([P, P], U32, name="w_first", align_bytes=64)
         w_second = keep.tile([P, P], U32, name="w_second", align_bytes=64)
@@ -59,7 +61,7 @@ def tile_attend_gdelta_kernel(tc, dyT, oT, wo_words, wo_scales, gq, offs, out_0,
         nc.gpsimd.memset(w_scales[:].bitcast(I32), 0)
 
         gate_table = keep.tile([P, T], F32, name="gate_table")
-        nc.gpsimd.memset(gate_table[:].bitcast(I32), 0)
+        nc.vector.memset(gate_table[:].bitcast(I32), 0)
         nc.scalar.copy(out=gate_table[0:1, :], in_=gate_line[:])
 
         o_tiles = [keep.tile([P, T], F32, name="o%d" % m) for m in range(TILES)]
@@ -83,7 +85,7 @@ def tile_attend_gdelta_kernel(tc, dyT, oT, wo_words, wo_scales, gq, offs, out_0,
 
         windows = [keep.tile([P, T], F32, name="window%d" % w) for w in range(WINDOWS)]
         for w in range(WINDOWS):
-            nc.gpsimd.memset(windows[w][:].bitcast(I32), 0)
+            (nc.vector if w == 0 else nc.gpsimd).memset(windows[w][:].bitcast(I32), 0)
 
         grouped = [keep.tile([P, HALF, PACK], BF16, name="grouped%d" % h, align_bytes=64) for h in range(2)]
         first_pair = keep.tile([P, 2, SLOTS], BF16, name="first_pair")
@@ -121,16 +123,15 @@ def tile_attend_gdelta_kernel(tc, dyT, oT, wo_words, wo_scales, gq, offs, out_0,
                 in_=grouped[h][:].rearrange("p s t -> p (s t)"),
             )
 
-        last = SLOTS - P
+        last = SLOTS - LATE * P
         picked = keep.tile([P, (TILES - 1) * SLOTS], F32, name="picked")
-        final = keep.tile([P, SLOTS + last], F32, name="final", tag="final")
-        picks = [picked[:, m * SLOTS : (m + 1) * SLOTS] for m in range(TILES - 1)] + [final[:, SLOTS:]]
+        final = keep.tile([P, last], F32, name="final", tag="final")
+        picks = [picked[:, m * SLOTS : (m + 1) * SLOTS] for m in range(TILES - 1)] + [final[:]]
         back = keep.tile([P, TILES * SLOTS], F32, name="back")
         slab = [slice(m * SLOTS, (m + 1) * SLOTS) for m in range(TILES)]
         nc.vector.tensor_copy(picked[:, slab[0]], o_tiles[0][:].indirect(offsets[:]))
 
-        grads = {m: keep.tile([P, SLOTS], F32, name="grad%d" % m)[:] for m in range(FUSED, TILES - 1)}
-        grads[TILES - 1] = final[:, 0:SLOTS]
+        grads = {m: keep.tile([P, SLOTS], F32, name="grad%d" % m)[:] for m in range(FUSED, TILES)}
         for m in range(TILES):
             cols = slice(m * P, (m + 1) * P)
             prod = psum.tile([P, SLOTS], F32, name="prod", tag="prod%d" % m)
@@ -171,11 +172,16 @@ def tile_attend_gdelta_kernel(tc, dyT, oT, wo_words, wo_scales, gq, offs, out_0,
                 nc.gpsimd.tensor_tensor(terms, picks[m], back[:, cols], MULT)
             blocks = [terms[:, j * P : (j + 1) * P] for j in range(width // P)]
             if m == TILES - 1:
-                tail = keep.tile([P, P], F32, name="tail", tag="final")
-                nc.vector.tensor_tensor(
-                    tail[:], o_tiles[m][:].indirect(offsets[:, last // PER_COLUMN :]), back[:, m * SLOTS + last :], MULT
-                )
-                blocks.append(tail[:])
+                tail = keep.tile([P, LATE * P], F32, name="tail", tag="final")
+                for j in range(LATE):
+                    lo = last + j * P
+                    nc.vector.tensor_tensor(
+                        tail[:, j * P : (j + 1) * P],
+                        o_tiles[m][:].indirect(offsets[:, lo // PER_COLUMN : (lo + P) // PER_COLUMN]),
+                        back[:, m * SLOTS + lo : m * SLOTS + lo + P],
+                        MULT,
+                    )
+                    blocks.append(tail[:, j * P : (j + 1) * P])
             for j in range(BLOCKS):
                 nc.tensor.matmul(
                     sums[j][:], lhsT=blocks[j], rhs=ident[:], is_transpose=True, start=(m == 0), stop=(m == TILES - 1)
@@ -192,7 +198,7 @@ def tile_attend_gdelta_kernel(tc, dyT, oT, wo_words, wo_scales, gq, offs, out_0,
                 )
         delta_rows = keep.tile([P, P], F32, name="delta_rows", align_bytes=64)
         nc.vector.transpose(delta_rows[:], delta_cols[:])
-        nc.sync.dma_start(
+        nc.scalar.dma_start(
             out=out_1[0].rearrange("(j q r) -> q j r", j=BLOCKS, r=QUAD),
             in_=delta_rows[0:P:QUAD, :].rearrange("q (j r) -> q j r", r=QUAD),
         )

@@ -14,6 +14,7 @@ PER_COLUMN = 16
 WINDOWS = 4
 FUSED = 2
 LATE = 2
+CUT = 3 * T // 4
 HALF = SLOTS // 2
 
 FLOPS = 2 * D * E * SLOTS
@@ -53,8 +54,8 @@ def tile_attend_gdelta_kernel(tc, dyT, oT, wo_words, wo_scales, gq, offs, out_0,
 
         w_first = keep.tile([P, P], U32, name="w_first", align_bytes=64)
         w_second = keep.tile([P, P], U32, name="w_second", align_bytes=64)
-        w_rest = keep.tile([P, E - 2 * P], U32, name="w_rest", align_bytes=64)
-        w_tiles = [w_first[:], w_second[:], w_rest[:, 0:P], w_rest[:, P:]]
+        w_rest = [keep.tile([P, P], U32, name="w%d" % m, align_bytes=64) for m in range(FUSED, TILES)]
+        w_tiles = [w_first[:], w_second[:], w_rest[0][:], w_rest[1][:]]
         w_dram = wo_words[0].rearrange("p n t -> p (n t)").bitcast(I32)
 
         w_scales = keep.tile([P, E], U8, name="w_scales", align_bytes=64)
@@ -71,12 +72,15 @@ def tile_attend_gdelta_kernel(tc, dyT, oT, wo_words, wo_scales, gq, offs, out_0,
                 in_=wo_scales[0, 4 * quad : 4 * quad + 4, :].bitcast(I32),
             )
         for m in range(TILES):
-            nc.sync.dma_start(out=o_tiles[m][:], in_=oT[m * P : (m + 1) * P, :])
+            if m > 0:
+                nc.sync.dma_start(out=o_tiles[m][:], in_=oT[m * P : (m + 1) * P, :])
             if m == 0:
+                nc.sync.dma_start(out=o_tiles[0][:, 0:CUT], in_=oT[0:P, 0:CUT])
                 nc.sync.dma_start(out=w_first[:].bitcast(I32), in_=w_dram[:, 0:P])
+                nc.sync.dma_start(out=o_tiles[0][:, CUT:], in_=oT[0:P, CUT:])
                 nc.sync.dma_start(out=w_second[:].bitcast(I32), in_=w_dram[:, P : 2 * P])
-            if m == 2:
-                nc.sync.dma_start(out=w_rest[:].bitcast(I32), in_=w_dram[:, 2 * P :])
+            if m >= FUSED:
+                nc.sync.dma_start(out=w_tiles[m].bitcast(I32), in_=w_dram[:, m * P : (m + 1) * P])
 
         ident = keep.tile([P, P], F32, name="ident")
         make_identity(nc, ident[:])
@@ -160,16 +164,12 @@ def tile_attend_gdelta_kernel(tc, dyT, oT, wo_words, wo_scales, gq, offs, out_0,
             nc.sync.dma_start(out=out_0[m * P : (m + 1) * P, :], in_=window[:])
 
         sums = [psum.tile([P, P], F32, name="sum%d" % j, tag="sum%d" % j) for j in range(BLOCKS)]
-        early = keep.tile([P, FUSED * SLOTS], F32, name="early", tag="gate")
-        nc.gpsimd.tensor_tensor(early[:], picked[:, 0 : FUSED * SLOTS], back[:, 0 : FUSED * SLOTS], MULT)
+        all_terms = keep.tile([P, TILES * SLOTS - LATE * P], F32, name="all_terms", tag="gate")
         for m in range(TILES):
             width = SLOTS if m < TILES - 1 else last
-            if m < FUSED:
-                terms = early[:, slab[m]]
-            else:
-                terms = keep.tile([P, width], F32, name="terms%d" % m)[:]
-                cols = slice(m * SLOTS, m * SLOTS + width)
-                nc.gpsimd.tensor_tensor(terms, picks[m], back[:, cols], MULT)
+            cols = slice(m * SLOTS, m * SLOTS + width)
+            terms = all_terms[:, cols]
+            nc.gpsimd.tensor_tensor(terms, picks[m], back[:, cols], MULT)
             blocks = [terms[:, j * P : (j + 1) * P] for j in range(width // P)]
             if m == TILES - 1:
                 tail = keep.tile([P, LATE * P], F32, name="tail", tag="final")

@@ -63,7 +63,7 @@ def tile_attend_gdelta_kernel(tc, dyT, oT, wo_words, wo_scales, gq, offs, out_0,
 
         gate_table = keep.tile([P, T], F32, name="gate_table")
         nc.vector.memset(gate_table[:].bitcast(I32), 0)
-        nc.scalar.copy(out=gate_table[0:1, :], in_=gate_line[:])
+        nc.vector.tensor_copy(gate_table[0:1, :], gate_line[:])
 
         o_tiles = [keep.tile([P, T], F32, name="o%d" % m) for m in range(TILES)]
         for quad in range(P // QUAD):
@@ -112,15 +112,19 @@ def tile_attend_gdelta_kernel(tc, dyT, oT, wo_words, wo_scales, gq, offs, out_0,
             nc.tensor.transpose(gate_spread[:, j, :], gate_cols[:, j : j + 1].to_broadcast([P, P]), ident[:])
         gate = keep.tile([P, SLOTS], F32, name="gate", tag="gate")
         nc.scalar.copy(out=gate[:], in_=gate_spread[:].rearrange("p j s -> p (j s)"))
+        gate_second = keep.tile([P, HALF], F32, name="gate_second", tag="gate_second")
+        nc.scalar.copy(out=gate_second[:], in_=gate_spread[:].rearrange("p j s -> p (j s)")[:, HALF:])
 
         for t in range(2, PACK):
             for h in range(2):
                 nc.vector.tensor_copy(grouped[h][:, :, t], dy_planes[t][:].indirect(half_lists[h]))
 
-        dy_words = keep.tile([P, SLOTS], U32, name="dy_words", align_bytes=64)
-        dy_scales = keep.tile([P, SLOTS], U8, name="dy_scales", align_bytes=64)
+        dy_words = keep.tile([P, HALF + SLOTS], U32, name="dy_words", align_bytes=64)
+        dy_scales = keep.tile([P, HALF + SLOTS], U8, name="dy_scales", align_bytes=64)
+        nc.gpsimd.memset(dy_words[:, 0:HALF].bitcast(I32), 0)
+        nc.gpsimd.memset(dy_scales[:, 0:HALF].bitcast(I32), 0)
         for h in range(2):
-            half = slice(h * HALF, (h + 1) * HALF)
+            half = slice((h + 1) * HALF, (h + 2) * HALF)
             nc.vector.quantize_mx(
                 out=dy_words[:, half].bitcast(E5M2),
                 scales=dy_scales[:, half],
@@ -135,26 +139,37 @@ def tile_attend_gdelta_kernel(tc, dyT, oT, wo_words, wo_scales, gq, offs, out_0,
         slab = [slice(m * SLOTS, (m + 1) * SLOTS) for m in range(TILES)]
         nc.vector.tensor_copy(picked[:, slab[0]], o_tiles[0][:].indirect(offsets[:]))
 
-        grads = {m: keep.tile([P, SLOTS], F32, name="grad%d" % m)[:] for m in range(FUSED, TILES)}
-        for m in range(TILES):
-            cols = slice(m * P, (m + 1) * P)
-            prod = psum.tile([P, SLOTS], F32, name="prod", tag="prod%d" % m)
+        def product(m, first, bank):
+            prod = psum.tile([P, SLOTS], F32, name="prod", tag="prod%d" % bank)
             nc.tensor.matmul_mx(
                 out=prod[:],
                 lhsT=w_tiles[m].bitcast(E4M3),
-                lhsT_scale=w_scales[:, cols],
-                rhs=dy_words[:].bitcast(E5M2),
-                rhs_scale=dy_scales[:],
+                lhsT_scale=w_scales[:, m * P : (m + 1) * P],
+                rhs=dy_words[:, first : first + SLOTS].bitcast(E5M2),
+                rhs_scale=dy_scales[:, first : first + SLOTS],
                 start=True,
                 stop=True,
             )
-            nc.scalar.copy(out=back[:, slab[m]], in_=prod[:])
-            if m >= FUSED:
-                nc.gpsimd.tensor_tensor(grads[m], back[:, slab[m]], gate[:], MULT)
+            return prod
 
-        for m in range(FUSED):
-            nc.vector.tensor_tensor(windows[m][:].indirect(offsets[:]), back[:, slab[m]], gate[:], MULT)
-            nc.sync.dma_start(out=out_0[m * P : (m + 1) * P, :], in_=windows[m][:])
+        nc.scalar.copy(out=back[:, 0:HALF], in_=product(0, 0, 0)[:, HALF:])
+        nc.scalar.copy(out=back[:, slab[1]], in_=product(1, HALF, 1)[:])
+        nc.scalar.copy(out=back[:, HALF:SLOTS], in_=product(0, HALF, 1)[:, HALF:])
+
+        nc.vector.tensor_tensor(windows[0][:].indirect(half_lists[0]), back[:, 0:HALF], gate[:, 0:HALF], MULT)
+        nc.vector.tensor_tensor(windows[1][:].indirect(offsets[:]), back[:, slab[1]], gate[:], MULT)
+        nc.sync.dma_start(out=out_0[P : 2 * P, :], in_=windows[1][:])
+        nc.vector.tensor_tensor(windows[0][:].indirect(half_lists[1]), back[:, HALF:SLOTS], gate_second[:], MULT)
+        nc.sync.dma_start(out=out_0[0:P, :], in_=windows[0][:])
+
+        grads = {
+            m: keep.tile([P, SLOTS], F32, name="grad%d" % m, tag="gate_second" if m == FUSED else "grad")[:]
+            for m in range(FUSED, TILES)
+        }
+        for m in range(FUSED, TILES):
+            nc.scalar.copy(out=back[:, slab[m]], in_=product(m, HALF, m)[:])
+            nc.gpsimd.tensor_tensor(grads[m], back[:, slab[m]], gate[:], MULT)
+
         for m in range(1, TILES):
             width = SLOTS if m < TILES - 1 else last
             nc.vector.tensor_copy(picks[m], o_tiles[m][:].indirect(offsets[:, 0 : width // PER_COLUMN]))

@@ -14,7 +14,6 @@ PER_COLUMN = 16
 WINDOWS = 4
 FUSED = 2
 LATE = 2
-CUT = 3 * T // 4
 HALF = SLOTS // 2
 
 FLOPS = 2 * D * E * SLOTS
@@ -67,7 +66,7 @@ def tile_attend_gdelta_kernel(tc, dyT, oT, wo_words, wo_scales, gq, offs, out_0,
 
         o_tiles = [keep.tile([P, T], F32, name="o%d" % m) for m in range(TILES)]
         for quad in range(P // QUAD):
-            nc.sync.dma_start(
+            nc.scalar.dma_start(
                 out=w_scales[QUAD * quad : QUAD * quad + 4, :].bitcast(I32),
                 in_=wo_scales[0, 4 * quad : 4 * quad + 4, :].bitcast(I32),
             )
@@ -75,9 +74,8 @@ def tile_attend_gdelta_kernel(tc, dyT, oT, wo_words, wo_scales, gq, offs, out_0,
             if m > 0:
                 nc.sync.dma_start(out=o_tiles[m][:], in_=oT[m * P : (m + 1) * P, :])
             if m == 0:
-                nc.sync.dma_start(out=o_tiles[0][:, 0:CUT], in_=oT[0:P, 0:CUT])
                 nc.sync.dma_start(out=w_first[:].bitcast(I32), in_=w_dram[:, 0:P])
-                nc.sync.dma_start(out=o_tiles[0][:, CUT:], in_=oT[0:P, CUT:])
+                nc.sync.dma_start(out=o_tiles[0][:], in_=oT[0:P, :])
                 nc.sync.dma_start(out=w_second[:].bitcast(I32), in_=w_dram[:, P : 2 * P])
             if m >= FUSED:
                 nc.sync.dma_start(out=w_tiles[m].bitcast(I32), in_=w_dram[:, m * P : (m + 1) * P])

@@ -11,10 +11,10 @@ BLOCKS = SLOTS // P
 BANK = 512
 QUAD = 32
 PER_COLUMN = 16
-WINDOWS = 4
 FUSED = 2
 LATE = 2
 HALF = SLOTS // 2
+CUT = 3 * T // 4
 
 FLOPS = 2 * D * E * SLOTS
 BYTES = 4 * (D * T + 2 * E * T + T + SLOTS) + D * E + D * E // 32 + 2 * P * SLOTS // 16
@@ -64,7 +64,7 @@ def tile_attend_gdelta_kernel(tc, dyT, oT, wo_words, wo_scales, gq, offs, out_0,
         nc.vector.memset(gate_table[:].bitcast(I32), 0)
         nc.vector.tensor_copy(gate_table[0:1, :], gate_line[:])
 
-        o_tiles = [keep.tile([P, T], F32, name="o%d" % m) for m in range(TILES)]
+        o_tiles = [keep.tile([P, T], F32, name="o%d" % m, tag="o%d" % m) for m in range(TILES)]
         for quad in range(P // QUAD):
             nc.scalar.dma_start(
                 out=w_scales[QUAD * quad : QUAD * quad + 4, :].bitcast(I32),
@@ -74,8 +74,9 @@ def tile_attend_gdelta_kernel(tc, dyT, oT, wo_words, wo_scales, gq, offs, out_0,
             if m > 0:
                 nc.sync.dma_start(out=o_tiles[m][:], in_=oT[m * P : (m + 1) * P, :])
             if m == 0:
+                nc.sync.dma_start(out=o_tiles[0][:, 0:CUT], in_=oT[0:P, 0:CUT])
                 nc.sync.dma_start(out=w_first[:].bitcast(I32), in_=w_dram[:, 0:P])
-                nc.sync.dma_start(out=o_tiles[0][:], in_=oT[0:P, :])
+                nc.sync.dma_start(out=o_tiles[0][:, CUT:], in_=oT[0:P, CUT:])
                 nc.sync.dma_start(out=w_second[:].bitcast(I32), in_=w_dram[:, P : 2 * P])
             if m >= FUSED:
                 nc.sync.dma_start(out=w_tiles[m].bitcast(I32), in_=w_dram[:, m * P : (m + 1) * P])
@@ -85,11 +86,11 @@ def tile_attend_gdelta_kernel(tc, dyT, oT, wo_words, wo_scales, gq, offs, out_0,
         delta_cols = keep.tile([P, P], F32, name="delta_cols", align_bytes=64)
         nc.gpsimd.memset(delta_cols[:], 0.0)
 
-        windows = [keep.tile([P, T], F32, name="window%d" % w) for w in range(WINDOWS)]
-        for w in range(WINDOWS):
-            (nc.vector if w == 0 else nc.gpsimd).memset(windows[w][:].bitcast(I32), 0)
+        windows = [keep.tile([P, T], F32, name="window%d" % w) for w in range(FUSED)]
+        nc.vector.memset(windows[0][:].bitcast(I32), 0)
+        nc.gpsimd.memset(windows[1][:].bitcast(I32), 0)
 
-        grouped = [keep.tile([P, HALF, PACK], BF16, name="grouped%d" % h, align_bytes=64) for h in range(2)]
+        grouped = [keep.tile([P, HALF, PACK], BF16, name="grouped%d" % h, tag="grouped%d" % h, align_bytes=64) for h in range(2)]
         first_pair = keep.tile([P, 2, SLOTS], BF16, name="first_pair")
         for t in range(2):
             nc.vector.tensor_copy(first_pair[:, t, :], dy_planes[t][:].indirect(offsets[:]))
@@ -137,6 +138,11 @@ def tile_attend_gdelta_kernel(tc, dyT, oT, wo_words, wo_scales, gq, offs, out_0,
         slab = [slice(m * SLOTS, (m + 1) * SLOTS) for m in range(TILES)]
         nc.vector.tensor_copy(picked[:, slab[0]], o_tiles[0][:].indirect(offsets[:]))
 
+        windows.append(keep.tile([P, T], F32, name="window2", tag="grouped1", align_bytes=64))
+        windows.append(keep.tile([P, T], F32, name="window3", tag="o0"))
+        for w in range(FUSED, TILES):
+            nc.gpsimd.memset(windows[w][:].bitcast(I32), 0)
+
         def product(m, first, bank):
             prod = psum.tile([P, SLOTS], F32, name="prod", tag="prod%d" % bank)
             nc.tensor.matmul_mx(
@@ -172,7 +178,7 @@ def tile_attend_gdelta_kernel(tc, dyT, oT, wo_words, wo_scales, gq, offs, out_0,
             width = SLOTS if m < TILES - 1 else last
             nc.vector.tensor_copy(picks[m], o_tiles[m][:].indirect(offsets[:, 0 : width // PER_COLUMN]))
         for m in range(FUSED, TILES):
-            window = windows[m % WINDOWS]
+            window = windows[m]
             nc.vector.tensor_copy(window[:].indirect(offsets[:]), grads[m])
             nc.sync.dma_start(out=out_0[m * P : (m + 1) * P, :], in_=window[:])
 

@@ -12,7 +12,6 @@ BANK = 512
 QUAD = 32
 PER_COLUMN = 16
 FUSED = 2
-LATE = 2
 HALF = SLOTS // 2
 CUT = 3 * T // 4
 
@@ -130,10 +129,10 @@ def tile_attend_gdelta_kernel(tc, dyT, oT, wo_words, wo_scales, gq, offs, out_0,
                 in_=grouped[h][:].rearrange("p s t -> p (s t)"),
             )
 
-        last = SLOTS - LATE * P
+        early = [SLOTS - max(0, m - 1) * P for m in range(TILES)]
         picked = keep.tile([P, (TILES - 1) * SLOTS], F32, name="picked")
-        final = keep.tile([P, last], F32, name="final", tag="final")
-        picks = [picked[:, m * SLOTS : (m + 1) * SLOTS] for m in range(TILES - 1)] + [final[:]]
+        final = keep.tile([P, early[TILES - 1]], F32, name="final", tag="final")
+        picks = [picked[:, m * SLOTS : m * SLOTS + early[m]] for m in range(TILES - 1)] + [final[:]]
         back = keep.tile([P, TILES * SLOTS], F32, name="back")
         slab = [slice(m * SLOTS, (m + 1) * SLOTS) for m in range(TILES)]
         nc.vector.tensor_copy(picked[:, slab[0]], o_tiles[0][:].indirect(offsets[:]))
@@ -175,36 +174,36 @@ def tile_attend_gdelta_kernel(tc, dyT, oT, wo_words, wo_scales, gq, offs, out_0,
             nc.gpsimd.tensor_tensor(grads[m], back[:, slab[m]], gate[:], MULT)
 
         for m in range(1, TILES):
-            width = SLOTS if m < TILES - 1 else last
-            nc.vector.tensor_copy(picks[m], o_tiles[m][:].indirect(offsets[:, 0 : width // PER_COLUMN]))
+            nc.vector.tensor_copy(picks[m], o_tiles[m][:].indirect(offsets[:, 0 : early[m] // PER_COLUMN]))
         for m in range(FUSED, TILES):
             window = windows[m]
             nc.vector.tensor_copy(window[:].indirect(offsets[:]), grads[m])
             nc.sync.dma_start(out=out_0[m * P : (m + 1) * P, :], in_=window[:])
 
         sums = [psum.tile([P, P], F32, name="sum%d" % j, tag="sum%d" % j) for j in range(BLOCKS)]
-        all_terms = keep.tile([P, TILES * SLOTS - LATE * P], F32, name="all_terms", tag="gate")
+        all_terms = keep.tile([P, TILES * SLOTS], F32, name="all_terms", tag="gate")
+
+        def add_turned(m, j, block):
+            nc.tensor.matmul(
+                sums[j][:], lhsT=block, rhs=ident[:], is_transpose=True, start=(m == 0), stop=(m == TILES - 1)
+            )
+
         for m in range(TILES):
-            width = SLOTS if m < TILES - 1 else last
-            cols = slice(m * SLOTS, m * SLOTS + width)
-            terms = all_terms[:, cols]
-            nc.gpsimd.tensor_tensor(terms, picks[m], back[:, cols], MULT)
-            blocks = [terms[:, j * P : (j + 1) * P] for j in range(width // P)]
-            if m == TILES - 1:
-                tail = keep.tile([P, LATE * P], F32, name="tail", tag="final")
-                for j in range(LATE):
-                    lo = last + j * P
-                    nc.vector.tensor_tensor(
-                        tail[:, j * P : (j + 1) * P],
-                        o_tiles[m][:].indirect(offsets[:, lo // PER_COLUMN : (lo + P) // PER_COLUMN]),
-                        back[:, m * SLOTS + lo : m * SLOTS + lo + P],
-                        MULT,
-                    )
-                    blocks.append(tail[:, j * P : (j + 1) * P])
-            for j in range(BLOCKS):
-                nc.tensor.matmul(
-                    sums[j][:], lhsT=blocks[j], rhs=ident[:], is_transpose=True, start=(m == 0), stop=(m == TILES - 1)
-                )
+            cols = slice(m * SLOTS, m * SLOTS + early[m])
+            nc.gpsimd.tensor_tensor(all_terms[:, cols], picks[m], back[:, cols], MULT)
+            for j in range(early[m] // P):
+                add_turned(m, j, all_terms[:, m * SLOTS + j * P : m * SLOTS + (j + 1) * P])
+
+        late = [(m, j) for m in range(TILES) for j in range(early[m] // P, BLOCKS)]
+        tail = keep.tile([P, len(late) * P], F32, name="tail", tag="final")
+        for n, (m, j) in enumerate(late):
+            nc.vector.tensor_tensor(
+                tail[:, n * P : (n + 1) * P],
+                o_tiles[m][:].indirect(offsets[:, j * P // PER_COLUMN : (j + 1) * P // PER_COLUMN]),
+                back[:, m * SLOTS + j * P : m * SLOTS + (j + 1) * P],
+                MULT,
+            )
+            add_turned(m, j, tail[:, n * P : (n + 1) * P])
 
         gated = keep.tile([P, BLOCKS, P], F32, name="gated")
         for j in range(BLOCKS):

@@ -27,7 +27,6 @@ U8 = mybir.dt.uint8
 E4M3 = mybir.dt.float8_e4m3fn_x4
 E5M2 = mybir.dt.float8_e5m2_x4
 MULT = mybir.AluOpType.mult
-ADD = mybir.AluOpType.add
 COPY = mybir.ActivationFunctionType.Copy
 
 
@@ -183,40 +182,40 @@ def tile_attend_gdelta_kernel(tc, dyT, oT, wo_words, wo_scales, gq, offs, out_0,
         sums = [psum.tile([P, P], F32, name="sum%d" % j, tag="sum%d" % j) for j in range(BLOCKS)]
         all_terms = keep.tile([P, TILES * SLOTS], F32, name="all_terms", tag="gate")
 
-        def add_turned(m, j, block):
-            nc.tensor.matmul(
-                sums[j][:], lhsT=block, rhs=ident[:], is_transpose=True, start=(m == 0), stop=(m == TILES - 1)
-            )
+        added = [0] * BLOCKS
+
+        def add_turned(j, block):
+            first, last = added[j] == 0, added[j] == TILES - 1
+            nc.tensor.matmul(sums[j][:], lhsT=block, rhs=ident[:], is_transpose=True, start=first, stop=last)
+            added[j] = added[j] + 1
 
         for m in range(TILES):
             cols = slice(m * SLOTS, m * SLOTS + early[m])
             nc.gpsimd.tensor_tensor(all_terms[:, cols], picks[m], back[:, cols], MULT)
             for j in range(early[m] // P):
-                add_turned(m, j, all_terms[:, m * SLOTS + j * P : m * SLOTS + (j + 1) * P])
+                add_turned(j, all_terms[:, m * SLOTS + j * P : m * SLOTS + (j + 1) * P])
 
-        late = [(m, j) for m in range(TILES) for j in range(early[m] // P, BLOCKS)]
-        tail = keep.tile([P, len(late) * P], F32, name="tail", tag="final")
-        for n, (m, j) in enumerate(late):
+        tail = keep.tile([P, TILES * SLOTS - sum(early)], F32, name="tail", tag="final")
+        used = 0
+        for m in range(TILES - 1, FUSED - 1, -1):
+            width = SLOTS - early[m]
             nc.vector.tensor_tensor(
-                tail[:, n * P : (n + 1) * P],
-                o_tiles[m][:].indirect(offsets[:, j * P // PER_COLUMN : (j + 1) * P // PER_COLUMN]),
-                back[:, m * SLOTS + j * P : m * SLOTS + (j + 1) * P],
+                tail[:, used : used + width],
+                o_tiles[m][:].indirect(offsets[:, early[m] // PER_COLUMN :]),
+                back[:, m * SLOTS + early[m] : (m + 1) * SLOTS],
                 MULT,
             )
-            add_turned(m, j, tail[:, n * P : (n + 1) * P])
+            for j in range(early[m] // P, BLOCKS):
+                add_turned(j, tail[:, used : used + P])
+                used = used + P
 
         gated = keep.tile([P, BLOCKS, P], F32, name="gated")
         for j in range(BLOCKS):
             delta_j = delta_cols[:, QUAD * j : QUAD * j + 1]
-            if j < BLOCKS - 1:
-                nc.scalar.activation(gated[:, j, :], sums[j][:], COPY, scale=gate_cols[:, j : j + 1], accum_out=delta_j)
-            else:
-                nc.vector.tensor_scalar(
-                    gated[:, j, :], sums[j][:], gate_cols[:, j : j + 1], None, MULT, ADD, accum_out=delta_j
-                )
+            nc.scalar.activation(gated[:, j, :], sums[j][:], COPY, scale=gate_cols[:, j : j + 1], accum_out=delta_j)
         delta_rows = keep.tile([P, P], F32, name="delta_rows", align_bytes=64)
         nc.vector.transpose(delta_rows[:], delta_cols[:])
-        nc.scalar.dma_start(
+        nc.sync.dma_start(
             out=out_1[0].rearrange("(j q r) -> q j r", j=BLOCKS, r=QUAD),
             in_=delta_rows[0:P:QUAD, :].rearrange("q (j r) -> q j r", r=QUAD),
         )

@@ -6,14 +6,11 @@ from concourse.masks import make_identity
 D, E, SLOTS, T = 512, 512, 512, 2048
 P = 128
 PACK = 4
-TILES = E // P
+SLABS = E // P
 BLOCKS = SLOTS // P
-BANK = 512
 QUAD = 32
 PER_COLUMN = 16
-FUSED = 2
 HALF = SLOTS // 2
-CUT = 3 * T // 4
 
 FLOPS = 2 * D * E * SLOTS
 BYTES = 4 * (D * T + 2 * E * T + T + SLOTS) + D * E + D * E // 32 + 2 * P * SLOTS // 16
@@ -37,65 +34,47 @@ def tile_attend_gdelta_kernel(tc, dyT, oT, wo_words, wo_scales, gq, offs, out_0,
         psum = ctx.enter_context(tc.psum_pool(name="psum", bufs=1))
 
         offsets = keep.tile([P, SLOTS // PER_COLUMN], U16, name="offsets")
+        halves = [slice(h * HALF, (h + 1) * HALF) for h in range(2)]
         half_lists = [offsets[:, h * HALF // PER_COLUMN : (h + 1) * HALF // PER_COLUMN] for h in range(2)]
 
-        gate_line = keep.tile([1, T], F32, name="gate_line")
-        nc.scalar.dma_start(out=gate_line[:], in_=gq[0:1, :])
+        w_scales = keep.tile([P, E], U8, name="w_scales", align_bytes=64)
+        nc.gpsimd.memset(w_scales[:].bitcast(I32), 0)
+        gate_line = keep.tile([1, T], F32, name="gate_line", tag="line")
+        nc.sync.dma_start(out=gate_line[:], in_=gq[0:1, :])
 
-        dy_planes = [keep.tile([P, T], F32, name="dy%d" % t) for t in range(PACK)]
+        dy_planes = [keep.tile([P, T], F32, name="dy%d" % t, tag="wide%d" % t) for t in range(PACK)]
         dy_rows = dyT.rearrange("(p t) w -> t p w", t=PACK)
         for t in range(PACK):
             nc.sync.dma_start(out=dy_planes[t][:], in_=dy_rows[t])
             if t == 0:
                 nc.sync.dma_start(offsets[:], offs)
-
-        w_first = keep.tile([P, P], U32, name="w_first", align_bytes=64)
-        w_second = keep.tile([P, P], U32, name="w_second", align_bytes=64)
-        w_rest = [keep.tile([P, P], U32, name="w%d" % m, align_bytes=64) for m in range(FUSED, TILES)]
-        w_tiles = [w_first[:], w_second[:], w_rest[0][:], w_rest[1][:]]
-        w_dram = wo_words[0].rearrange("p n t -> p (n t)").bitcast(I32)
-
-        w_scales = keep.tile([P, E], U8, name="w_scales", align_bytes=64)
-        nc.gpsimd.memset(w_scales[:].bitcast(I32), 0)
-
-        gate_table = keep.tile([P, T], F32, name="gate_table")
-        nc.vector.memset(gate_table[:].bitcast(I32), 0)
-        nc.vector.tensor_copy(gate_table[0:1, :], gate_line[:])
-
-        o_tiles = [keep.tile([P, T], F32, name="o%d" % m, tag="o%d" % m) for m in range(TILES)]
+        w_words = keep.tile([P, E], U32, name="w_words", align_bytes=64)
+        nc.sync.dma_start(out=w_words[:].bitcast(I32), in_=wo_words[0].rearrange("p n t -> p (n t)").bitcast(I32))
         for quad in range(P // QUAD):
-            nc.scalar.dma_start(
+            nc.sync.dma_start(
                 out=w_scales[QUAD * quad : QUAD * quad + 4, :].bitcast(I32),
                 in_=wo_scales[0, 4 * quad : 4 * quad + 4, :].bitcast(I32),
             )
-        for m in range(TILES):
-            if m > 0:
-                nc.sync.dma_start(out=o_tiles[m][:], in_=oT[m * P : (m + 1) * P, :])
-            if m == 0:
-                nc.sync.dma_start(out=o_tiles[0][:, 0:CUT], in_=oT[0:P, 0:CUT])
-                nc.sync.dma_start(out=w_first[:].bitcast(I32), in_=w_dram[:, 0:P])
-                nc.sync.dma_start(out=o_tiles[0][:, CUT:], in_=oT[0:P, CUT:])
-                nc.sync.dma_start(out=w_second[:].bitcast(I32), in_=w_dram[:, P : 2 * P])
-            if m >= FUSED:
-                nc.sync.dma_start(out=w_tiles[m].bitcast(I32), in_=w_dram[:, m * P : (m + 1) * P])
+        gate_table = keep.tile([P, T], F32, name="gate_table", tag="table")
+        nc.vector.memset(gate_table[:].bitcast(I32), 0)
 
         ident = keep.tile([P, P], F32, name="ident")
         make_identity(nc, ident[:])
         delta_cols = keep.tile([P, P], F32, name="delta_cols", align_bytes=64)
         nc.gpsimd.memset(delta_cols[:], 0.0)
+        nc.scalar.activation(gate_table[0:1, :], gate_line[:], COPY)
 
-        windows = [keep.tile([P, T], F32, name="window%d" % w) for w in range(FUSED)]
+        windows = [keep.tile([P, T], F32, name="window0")]
         nc.vector.memset(windows[0][:].bitcast(I32), 0)
+        windows.append(keep.tile([P, T], F32, name="window1", tag="line"))
         nc.gpsimd.memset(windows[1][:].bitcast(I32), 0)
 
         grouped = [keep.tile([P, HALF, PACK], BF16, name="grouped%d" % h, tag="grouped%d" % h, align_bytes=64) for h in range(2)]
         first_pair = keep.tile([P, 2, SLOTS], BF16, name="first_pair")
-        for t in range(2):
-            nc.vector.tensor_copy(first_pair[:, t, :], dy_planes[t][:].indirect(offsets[:]))
+        nc.vector.tensor_copy(first_pair[:, 0, :], dy_planes[0][:].indirect(offsets[:]))
+        nc.scalar.activation(first_pair[:, 1, :], dy_planes[1][:].indirect(offsets[:]), COPY)
         for h in range(2):
-            nc.scalar.copy(
-                out=grouped[h][:, :, 0:2], in_=first_pair[:, :, h * HALF : (h + 1) * HALF].rearrange("p t s -> p s t")
-            )
+            nc.scalar.copy(out=grouped[h][:, :, 0:2], in_=first_pair[:, :, halves[h]].rearrange("p t s -> p s t"))
 
         gate_row = keep.tile([P, SLOTS], F32, name="gate_row")
         nc.vector.tensor_copy(gate_row[:], gate_table[:].indirect(offsets[:]))
@@ -107,115 +86,91 @@ def tile_attend_gdelta_kernel(tc, dyT, oT, wo_words, wo_scales, gq, offs, out_0,
         gate_spread = psum.tile([P, BLOCKS, P], F32, name="gate_spread", tag="sum1")
         for j in range(BLOCKS):
             nc.tensor.transpose(gate_spread[:, j, :], gate_cols[:, j : j + 1].to_broadcast([P, P]), ident[:])
-        gate = keep.tile([P, SLOTS], F32, name="gate", tag="gate")
+        gate = keep.tile([P, SLOTS], F32, name="gate")
         nc.scalar.copy(out=gate[:], in_=gate_spread[:].rearrange("p j s -> p (j s)"))
-        gate_second = keep.tile([P, HALF], F32, name="gate_second", tag="gate_second")
-        nc.scalar.copy(out=gate_second[:], in_=gate_spread[:].rearrange("p j s -> p (j s)")[:, HALF:])
 
         for t in range(2, PACK):
             for h in range(2):
                 nc.vector.tensor_copy(grouped[h][:, :, t], dy_planes[t][:].indirect(half_lists[h]))
 
-        dy_words = keep.tile([P, HALF + SLOTS], U32, name="dy_words", align_bytes=64)
-        dy_scales = keep.tile([P, HALF + SLOTS], U8, name="dy_scales", align_bytes=64)
-        nc.gpsimd.memset(dy_words[:, 0:HALF].bitcast(I32), 0)
-        nc.gpsimd.memset(dy_scales[:, 0:HALF].bitcast(I32), 0)
+        o_tiles = [keep.tile([P, T], F32, name="o%d" % m, tag="wide%d" % m) for m in range(SLABS)]
+        for m in range(SLABS):
+            nc.sync.dma_start(out=o_tiles[m][:], in_=oT[m * P : (m + 1) * P, :])
+        windows.append(keep.tile([P, T], F32, name="window2", tag="table"))
+        nc.gpsimd.memset(windows[2][:].bitcast(I32), 0)
+
+        dy_words = keep.tile([P, SLOTS], U32, name="dy_words", align_bytes=64)
+        dy_scales = keep.tile([P, SLOTS], U8, name="dy_scales", align_bytes=64)
         for h in range(2):
-            half = slice((h + 1) * HALF, (h + 2) * HALF)
             nc.vector.quantize_mx(
-                out=dy_words[:, half].bitcast(E5M2),
-                scales=dy_scales[:, half],
+                out=dy_words[:, halves[h]].bitcast(E5M2),
+                scales=dy_scales[:, halves[h]],
                 in_=grouped[h][:].rearrange("p s t -> p (s t)"),
             )
 
-        early = [SLOTS - max(0, m - 1) * P for m in range(TILES)]
-        picked = keep.tile([P, (TILES - 1) * SLOTS], F32, name="picked")
-        final = keep.tile([P, early[TILES - 1]], F32, name="final", tag="final")
-        picks = [picked[:, m * SLOTS : m * SLOTS + early[m]] for m in range(TILES - 1)] + [final[:]]
-        back = keep.tile([P, TILES * SLOTS], F32, name="back")
-        slab = [slice(m * SLOTS, (m + 1) * SLOTS) for m in range(TILES)]
-        nc.vector.tensor_copy(picked[:, slab[0]], o_tiles[0][:].indirect(offsets[:]))
+        windows.append(keep.tile([P, T], F32, name="window3", tag="grouped1", align_bytes=64))
+        nc.gpsimd.memset(windows[3][:].bitcast(I32), 0)
 
-        windows.append(keep.tile([P, T], F32, name="window2", tag="grouped1", align_bytes=64))
-        windows.append(keep.tile([P, T], F32, name="window3", tag="o0"))
-        for w in range(FUSED, TILES):
-            nc.gpsimd.memset(windows[w][:].bitcast(I32), 0)
-
-        def product(m, first, bank):
-            prod = psum.tile([P, SLOTS], F32, name="prod", tag="prod%d" % bank)
+        grads = [keep.tile([P, SLOTS], F32, name="grad%d" % m) for m in range(SLABS)]
+        for m in range(SLABS):
+            prod = psum.tile([P, SLOTS], F32, name="prod", tag="prod%d" % m)
             nc.tensor.matmul_mx(
                 out=prod[:],
-                lhsT=w_tiles[m].bitcast(E4M3),
+                lhsT=w_words[:, m * P : (m + 1) * P].bitcast(E4M3),
                 lhsT_scale=w_scales[:, m * P : (m + 1) * P],
-                rhs=dy_words[:, first : first + SLOTS].bitcast(E5M2),
-                rhs_scale=dy_scales[:, first : first + SLOTS],
+                rhs=dy_words[:].bitcast(E5M2),
+                rhs_scale=dy_scales[:],
                 start=True,
                 stop=True,
             )
-            return prod
-
-        nc.scalar.copy(out=back[:, 0:HALF], in_=product(0, 0, 0)[:, HALF:])
-        nc.scalar.copy(out=back[:, slab[1]], in_=product(1, HALF, 1)[:])
-        nc.scalar.copy(out=back[:, HALF:SLOTS], in_=product(0, HALF, 1)[:, HALF:])
-
-        nc.vector.tensor_tensor(windows[0][:].indirect(half_lists[0]), back[:, 0:HALF], gate[:, 0:HALF], MULT)
-        nc.vector.tensor_tensor(windows[1][:].indirect(offsets[:]), back[:, slab[1]], gate[:], MULT)
-        nc.sync.dma_start(out=out_0[P : 2 * P, :], in_=windows[1][:])
-        nc.vector.tensor_tensor(windows[0][:].indirect(half_lists[1]), back[:, HALF:SLOTS], gate_second[:], MULT)
-        nc.sync.dma_start(out=out_0[0:P, :], in_=windows[0][:])
-
-        grads = {
-            m: keep.tile([P, SLOTS], F32, name="grad%d" % m, tag="gate_second" if m == FUSED else "grad")[:]
-            for m in range(FUSED, TILES)
-        }
-        for m in range(FUSED, TILES):
-            nc.scalar.copy(out=back[:, slab[m]], in_=product(m, HALF, m)[:])
-            nc.gpsimd.tensor_tensor(grads[m], back[:, slab[m]], gate[:], MULT)
-
-        for m in range(1, TILES):
-            nc.vector.tensor_copy(picks[m], o_tiles[m][:].indirect(offsets[:, 0 : early[m] // PER_COLUMN]))
-        for m in range(FUSED, TILES):
-            window = windows[m]
-            nc.vector.tensor_copy(window[:].indirect(offsets[:]), grads[m])
-            nc.sync.dma_start(out=out_0[m * P : (m + 1) * P, :], in_=window[:])
+            nc.vector.tensor_tensor(grads[m][:], prod[:], gate[:], MULT)
 
         sums = [psum.tile([P, P], F32, name="sum%d" % j, tag="sum%d" % j) for j in range(BLOCKS)]
-        all_terms = keep.tile([P, TILES * SLOTS], F32, name="all_terms", tag="gate")
+        terms = [keep.tile([P, SLOTS], F32, name="term%d" % m) for m in range(SLABS)]
 
-        added = [0] * BLOCKS
+        def place(m):
+            if m % 2 == 0:
+                for h in range(2):
+                    nc.scalar.activation(windows[m][:].indirect(half_lists[h]), grads[m][:, halves[h]], COPY)
+            else:
+                nc.vector.tensor_copy(windows[m][:].indirect(offsets[:]), grads[m][:])
+            nc.sync.dma_start(out=out_0[m * P : (m + 1) * P, :], in_=windows[m][:])
 
-        def add_turned(j, block):
-            first, last = added[j] == 0, added[j] == TILES - 1
-            nc.tensor.matmul(sums[j][:], lhsT=block, rhs=ident[:], is_transpose=True, start=first, stop=last)
-            added[j] = added[j] + 1
+        def add_turned(m, blocks):
+            for j in blocks:
+                nc.tensor.matmul(
+                    sums[j][:],
+                    lhsT=terms[m][:, j * P : (j + 1) * P],
+                    rhs=ident[:],
+                    is_transpose=True,
+                    start=m == 0,
+                    stop=m == SLABS - 1,
+                )
 
-        for m in range(TILES):
-            cols = slice(m * SLOTS, m * SLOTS + early[m])
-            nc.gpsimd.tensor_tensor(all_terms[:, cols], picks[m], back[:, cols], MULT)
-            for j in range(early[m] // P):
-                add_turned(j, all_terms[:, m * SLOTS + j * P : m * SLOTS + (j + 1) * P])
+        place(0)
+        place(1)
+        for m in range(2):
+            nc.vector.tensor_tensor(terms[m][:], o_tiles[m][:].indirect(offsets[:]), grads[m][:], MULT)
+            add_turned(m, range(BLOCKS))
+        place(2)
+        place(3)
+        picks = keep.tile([P, 2, SLOTS], F32, name="picks")
+        nc.scalar.activation(picks[:, 0, :], o_tiles[2][:].indirect(offsets[:]), COPY)
+        nc.gpsimd.tensor_tensor(terms[2][:], picks[:, 0, :], grads[2][:], MULT)
+        add_turned(2, range(BLOCKS))
+        for h in range(2):
+            nc.scalar.activation(picks[:, 1, halves[h]], o_tiles[3][:].indirect(half_lists[h]), COPY)
+            nc.gpsimd.tensor_tensor(terms[3][:, halves[h]], picks[:, 1, halves[h]], grads[3][:, halves[h]], MULT)
+            add_turned(3, range(2 * h, 2 * h + 2))
 
-        tail = keep.tile([P, TILES * SLOTS - sum(early)], F32, name="tail", tag="final")
-        used = 0
-        for m in range(TILES - 1, FUSED - 1, -1):
-            width = SLOTS - early[m]
-            nc.vector.tensor_tensor(
-                tail[:, used : used + width],
-                o_tiles[m][:].indirect(offsets[:, early[m] // PER_COLUMN :]),
-                back[:, m * SLOTS + early[m] : (m + 1) * SLOTS],
-                MULT,
-            )
-            for j in range(early[m] // P, BLOCKS):
-                add_turned(j, tail[:, used : used + P])
-                used = used + P
-
-        gated = keep.tile([P, BLOCKS, P], F32, name="gated")
+        spent = keep.tile([P, BLOCKS, P], F32, name="spent")
         for j in range(BLOCKS):
-            delta_j = delta_cols[:, QUAD * j : QUAD * j + 1]
-            nc.scalar.activation(gated[:, j, :], sums[j][:], COPY, scale=gate_cols[:, j : j + 1], accum_out=delta_j)
+            nc.scalar.activation(
+                spent[:, j, :], sums[j][:], COPY, accum_out=delta_cols[:, QUAD * j : QUAD * j + 1]
+            )
         delta_rows = keep.tile([P, P], F32, name="delta_rows", align_bytes=64)
         nc.vector.transpose(delta_rows[:], delta_cols[:])
-        nc.sync.dma_start(
+        nc.scalar.dma_start(
             out=out_1[0].rearrange("(j q r) -> q j r", j=BLOCKS, r=QUAD),
             in_=delta_rows[0:P:QUAD, :].rearrange("q (j r) -> q j r", r=QUAD),
         )

@@ -41,13 +41,12 @@ def tile_attend_gdelta_kernel(tc, dyT, oT, wo_words, wo_scales, gq, offs, out_0,
         nc.gpsimd.memset(w_scales[:].bitcast(I32), 0)
         gate_line = keep.tile([1, T], F32, name="gate_line", tag="line")
         nc.sync.dma_start(out=gate_line[:], in_=gq[0:1, :])
+        nc.sync.dma_start(offsets[:], offs)
 
         dy_planes = [keep.tile([P, T], F32, name="dy%d" % t, tag="wide%d" % t) for t in range(PACK)]
         dy_rows = dyT.rearrange("(p t) w -> t p w", t=PACK)
         for t in range(PACK):
             nc.sync.dma_start(out=dy_planes[t][:], in_=dy_rows[t])
-            if t == 0:
-                nc.sync.dma_start(offsets[:], offs)
         w_words = keep.tile([P, E], U32, name="w_words", align_bytes=64)
         nc.sync.dma_start(out=w_words[:].bitcast(I32), in_=wo_words[0].rearrange("p n t -> p (n t)").bitcast(I32))
         for quad in range(P // QUAD):
@@ -56,48 +55,51 @@ def tile_attend_gdelta_kernel(tc, dyT, oT, wo_words, wo_scales, gq, offs, out_0,
                 in_=wo_scales[0, 4 * quad : 4 * quad + 4, :].bitcast(I32),
             )
         gate_table = keep.tile([P, T], F32, name="gate_table", tag="table")
-        nc.vector.memset(gate_table[:].bitcast(I32), 0)
+        nc.gpsimd.memset(gate_table[:].bitcast(I32), 0)
+        nc.vector.tensor_copy(gate_table[0:1, :], gate_line[:])
 
         ident = keep.tile([P, P], F32, name="ident")
         make_identity(nc, ident[:])
         delta_cols = keep.tile([P, P], F32, name="delta_cols", align_bytes=64)
         nc.gpsimd.memset(delta_cols[:], 0.0)
-        nc.scalar.activation(gate_table[0:1, :], gate_line[:], COPY)
 
-        windows = [keep.tile([P, T], F32, name="window0")]
-        nc.vector.memset(windows[0][:].bitcast(I32), 0)
-        windows.append(keep.tile([P, T], F32, name="window1", tag="line"))
-        nc.gpsimd.memset(windows[1][:].bitcast(I32), 0)
+        windows = [keep.tile([P, T], F32, name="window0", tag="line")]
+        nc.gpsimd.memset(windows[0][:].bitcast(I32), 0)
 
-        grouped = [keep.tile([P, HALF, PACK], BF16, name="grouped%d" % h, tag="grouped%d" % h, align_bytes=64) for h in range(2)]
-        first_pair = keep.tile([P, 2, SLOTS], BF16, name="first_pair")
-        nc.vector.tensor_copy(first_pair[:, 0, :], dy_planes[0][:].indirect(offsets[:]))
-        nc.scalar.activation(first_pair[:, 1, :], dy_planes[1][:].indirect(offsets[:]), COPY)
-        for h in range(2):
-            nc.scalar.copy(out=grouped[h][:, :, 0:2], in_=first_pair[:, :, halves[h]].rearrange("p t s -> p s t"))
-
-        gate_row = keep.tile([P, SLOTS], F32, name="gate_row")
+        gate_row = keep.tile([P, SLOTS], F32, name="gate_row", tag="row")
         nc.vector.tensor_copy(gate_row[:], gate_table[:].indirect(offsets[:]))
-        gate_turned = psum.tile([P, BLOCKS, P], F32, name="gate_turned", tag="sum0")
+        gate_turned = psum.tile([P, BLOCKS, P], F32, name="gate_turned", tag="bank6")
         for j in range(BLOCKS):
             nc.tensor.transpose(gate_turned[:, j, :], gate_row[:, j * P : (j + 1) * P], ident[:])
         gate_cols = keep.tile([P, BLOCKS], F32, name="gate_cols")
-        nc.scalar.copy(out=gate_cols[:], in_=gate_turned[:, :, 0])
-        gate_spread = psum.tile([P, BLOCKS, P], F32, name="gate_spread", tag="sum1")
+        nc.scalar.activation(gate_cols[:], gate_turned[:, :, 0], COPY)
+        gate_spread = psum.tile([P, BLOCKS, P], F32, name="gate_spread", tag="bank7")
         for j in range(BLOCKS):
             nc.tensor.transpose(gate_spread[:, j, :], gate_cols[:, j : j + 1].to_broadcast([P, P]), ident[:])
         gate = keep.tile([P, SLOTS], F32, name="gate")
         nc.scalar.copy(out=gate[:], in_=gate_spread[:].rearrange("p j s -> p (j s)"))
+        windows.append(keep.tile([P, T], F32, name="window1", tag="table"))
+        windows.append(keep.tile([P, T], F32, name="window2", tag="row"))
+        for m in range(1, 3):
+            nc.gpsimd.memset(windows[m][:].bitcast(I32), 0)
 
+        grouped = [keep.tile([P, HALF, PACK], BF16, name="grouped%d" % h, tag="grouped%d" % h, align_bytes=64) for h in range(2)]
+        first_pair = keep.tile([P, 2, SLOTS], BF16, name="first_pair")
+        for t in range(2):
+            nc.vector.tensor_copy(first_pair[:, t, :], dy_planes[t][:].indirect(offsets[:]))
+        for h in range(2):
+            nc.scalar.copy(out=grouped[h][:, :, 0:2], in_=first_pair[:, :, halves[h]].rearrange("p t s -> p s t"))
+
+        second_pair = keep.tile([P, 2, HALF], BF16, name="second_pair")
+        nc.vector.tensor_copy(second_pair[:, 0, :], dy_planes[2][:].indirect(half_lists[1]))
         for t in range(2, PACK):
-            for h in range(2):
-                nc.vector.tensor_copy(grouped[h][:, :, t], dy_planes[t][:].indirect(half_lists[h]))
+            nc.vector.tensor_copy(grouped[0][:, :, t], dy_planes[t][:].indirect(half_lists[0]))
+        nc.scalar.activation(second_pair[:, 1, :], dy_planes[3][:].indirect(half_lists[1]), COPY)
+        nc.vector.tensor_copy(out=grouped[1][:, :, 2:4], in_=second_pair[:].rearrange("p t s -> p s t"))
 
         o_tiles = [keep.tile([P, T], F32, name="o%d" % m, tag="wide%d" % m) for m in range(SLABS)]
         for m in range(SLABS):
             nc.sync.dma_start(out=o_tiles[m][:], in_=oT[m * P : (m + 1) * P, :])
-        windows.append(keep.tile([P, T], F32, name="window2", tag="table"))
-        nc.gpsimd.memset(windows[2][:].bitcast(I32), 0)
 
         dy_words = keep.tile([P, SLOTS], U32, name="dy_words", align_bytes=64)
         dy_scales = keep.tile([P, SLOTS], U8, name="dy_scales", align_bytes=64)
@@ -112,32 +114,61 @@ def tile_attend_gdelta_kernel(tc, dyT, oT, wo_words, wo_scales, gq, offs, out_0,
         nc.gpsimd.memset(windows[3][:].bitcast(I32), 0)
 
         grads = [keep.tile([P, SLOTS], F32, name="grad%d" % m) for m in range(SLABS)]
-        for m in range(SLABS):
-            prod = psum.tile([P, SLOTS], F32, name="prod", tag="prod%d" % m)
+        picks = [keep.tile([P, SLOTS], F32, name="pick%d" % m) for m in range(SLABS)]
+        whole = slice(0, SLOTS)
+
+        def gated_product(m, slots, bank):
+            prod = psum.tile([P, slots.stop - slots.start], F32, name="prod", tag="bank%d" % bank)
             nc.tensor.matmul_mx(
                 out=prod[:],
                 lhsT=w_words[:, m * P : (m + 1) * P].bitcast(E4M3),
                 lhsT_scale=w_scales[:, m * P : (m + 1) * P],
-                rhs=dy_words[:].bitcast(E5M2),
-                rhs_scale=dy_scales[:],
+                rhs=dy_words[:, slots].bitcast(E5M2),
+                rhs_scale=dy_scales[:, slots],
                 start=True,
                 stop=True,
             )
-            nc.vector.tensor_tensor(grads[m][:], prod[:], gate[:], MULT)
+            nc.vector.tensor_tensor(grads[m][:, slots], prod[:], gate[:, slots], MULT)
 
-        sums = [psum.tile([P, P], F32, name="sum%d" % j, tag="sum%d" % j) for j in range(BLOCKS)]
-        terms = [keep.tile([P, SLOTS], F32, name="term%d" % m) for m in range(SLABS)]
+        def place_by_scalar(m, h):
+            nc.scalar.activation(windows[m][:].indirect(half_lists[h]), grads[m][:, halves[h]], COPY)
 
-        def place(m):
-            if m % 2 == 0:
-                for h in range(2):
-                    nc.scalar.activation(windows[m][:].indirect(half_lists[h]), grads[m][:, halves[h]], COPY)
-            else:
-                nc.vector.tensor_copy(windows[m][:].indirect(offsets[:]), grads[m][:])
+        def place_by_vector(m, h):
+            nc.vector.tensor_copy(windows[m][:].indirect(half_lists[h]), grads[m][:, halves[h]])
+
+        def store(m):
             nc.sync.dma_start(out=out_0[m * P : (m + 1) * P, :], in_=windows[m][:])
 
-        def add_turned(m, blocks):
-            for j in blocks:
+        def pick(m, slots):
+            entries = offsets[:, slots.start // PER_COLUMN : slots.stop // PER_COLUMN]
+            nc.scalar.activation(picks[m][:, slots], o_tiles[m][:].indirect(entries), COPY)
+
+        for h in range(2):
+            for m in range(2):
+                gated_product(m, halves[h], 2 * h + m)
+        for h in range(2):
+            place_by_scalar(0, h)
+        store(0)
+        nc.vector.tensor_copy(windows[1][:].indirect(offsets[:]), grads[1][:])
+        store(1)
+        pick(0, whole)
+        for m in range(SLABS - 1, 1, -1):
+            gated_product(m, whole, 2 + m)
+        pick(1, whole)
+        place_by_scalar(3, 0)
+        place_by_vector(3, 1)
+        store(3)
+        nc.vector.tensor_copy(windows[2][:].indirect(offsets[:]), grads[2][:])
+        store(2)
+        pick(2, whole)
+        pick(3, whole)
+
+        sums = [psum.tile([P, P], F32, name="sum%d" % j, tag="bank%d" % j) for j in range(BLOCKS)]
+        terms = [keep.tile([P, SLOTS], F32, name="term%d" % m) for m in range(SLABS)]
+        for m in range(SLABS):
+            engine = nc.vector if m == SLABS - 1 else nc.gpsimd
+            engine.tensor_tensor(terms[m][:], picks[m][:], grads[m][:], MULT)
+            for j in range(BLOCKS):
                 nc.tensor.matmul(
                     sums[j][:],
                     lhsT=terms[m][:, j * P : (j + 1) * P],
@@ -146,22 +177,6 @@ def tile_attend_gdelta_kernel(tc, dyT, oT, wo_words, wo_scales, gq, offs, out_0,
                     start=m == 0,
                     stop=m == SLABS - 1,
                 )
-
-        place(0)
-        place(1)
-        for m in range(2):
-            nc.vector.tensor_tensor(terms[m][:], o_tiles[m][:].indirect(offsets[:]), grads[m][:], MULT)
-            add_turned(m, range(BLOCKS))
-        place(2)
-        place(3)
-        picks = keep.tile([P, 2, SLOTS], F32, name="picks")
-        nc.scalar.activation(picks[:, 0, :], o_tiles[2][:].indirect(offsets[:]), COPY)
-        nc.gpsimd.tensor_tensor(terms[2][:], picks[:, 0, :], grads[2][:], MULT)
-        add_turned(2, range(BLOCKS))
-        for h in range(2):
-            nc.scalar.activation(picks[:, 1, halves[h]], o_tiles[3][:].indirect(half_lists[h]), COPY)
-            nc.gpsimd.tensor_tensor(terms[3][:, halves[h]], picks[:, 1, halves[h]], grads[3][:, halves[h]], MULT)
-            add_turned(3, range(2 * h, 2 * h + 2))
 
         spent = keep.tile([P, BLOCKS, P], F32, name="spent")
         for j in range(BLOCKS):

@@ -63,7 +63,7 @@ def tile_attend_gdelta_kernel(tc, dyT, oT, wo_words, wo_scales, gq, offs, out_0,
         delta_cols = keep.tile([P, P], F32, name="delta_cols", align_bytes=64)
         nc.gpsimd.memset(delta_cols[:], 0.0)
 
-        windows = [keep.tile([P, T], F32, name="window0", tag="line")]
+        windows = {0: keep.tile([P, T], F32, name="window0", tag="line")}
         nc.gpsimd.memset(windows[0][:].bitcast(I32), 0)
 
         gate_row = keep.tile([P, SLOTS], F32, name="gate_row", tag="row")
@@ -78,9 +78,9 @@ def tile_attend_gdelta_kernel(tc, dyT, oT, wo_words, wo_scales, gq, offs, out_0,
             nc.tensor.transpose(gate_spread[:, j, :], gate_cols[:, j : j + 1].to_broadcast([P, P]), ident[:])
         gate = keep.tile([P, SLOTS], F32, name="gate")
         nc.scalar.copy(out=gate[:], in_=gate_spread[:].rearrange("p j s -> p (j s)"))
-        windows.append(keep.tile([P, T], F32, name="window1", tag="table"))
-        windows.append(keep.tile([P, T], F32, name="window2", tag="row"))
-        for m in range(1, 3):
+        windows[1] = keep.tile([P, T], F32, name="window1", tag="table")
+        windows[2] = keep.tile([P, T], F32, name="window2", tag="row")
+        for m in (1, 2):
             nc.gpsimd.memset(windows[m][:].bitcast(I32), 0)
 
         grouped = [keep.tile([P, HALF, PACK], BF16, name="grouped%d" % h, tag="grouped%d" % h, align_bytes=64) for h in range(2)]
@@ -110,14 +110,14 @@ def tile_attend_gdelta_kernel(tc, dyT, oT, wo_words, wo_scales, gq, offs, out_0,
                 in_=grouped[h][:].rearrange("p s t -> p (s t)"),
             )
 
-        windows.append(keep.tile([P, T], F32, name="window3", tag="grouped1", align_bytes=64))
+        windows[3] = keep.tile([P, T], F32, name="window3", tag="grouped1", align_bytes=64)
         nc.gpsimd.memset(windows[3][:].bitcast(I32), 0)
 
         grads = [keep.tile([P, SLOTS], F32, name="grad%d" % m) for m in range(SLABS)]
         picks = [keep.tile([P, SLOTS], F32, name="pick%d" % m) for m in range(SLABS)]
         whole = slice(0, SLOTS)
 
-        def gated_product(m, slots, bank):
+        def product(m, slots, bank):
             prod = psum.tile([P, slots.stop - slots.start], F32, name="prod", tag="bank%d" % bank)
             nc.tensor.matmul_mx(
                 out=prod[:],
@@ -128,20 +128,22 @@ def tile_attend_gdelta_kernel(tc, dyT, oT, wo_words, wo_scales, gq, offs, out_0,
                 start=True,
                 stop=True,
             )
-            nc.vector.tensor_tensor(grads[m][:, slots], prod[:], gate[:, slots], MULT)
+            return prod
+
+        def gated_product(m, slots, bank):
+            nc.vector.tensor_tensor(grads[m][:, slots], product(m, slots, bank)[:], gate[:, slots], MULT)
 
         def place_by_scalar(m, h):
             nc.scalar.activation(windows[m][:].indirect(half_lists[h]), grads[m][:, halves[h]], COPY)
 
-        def place_by_vector(m, h):
-            nc.vector.tensor_copy(windows[m][:].indirect(half_lists[h]), grads[m][:, halves[h]])
+        def place_by_vector(m):
+            nc.vector.tensor_copy(windows[m][:].indirect(offsets[:]), grads[m][:])
 
         def store(m):
             nc.sync.dma_start(out=out_0[m * P : (m + 1) * P, :], in_=windows[m][:])
 
-        def pick(m, slots):
-            entries = offsets[:, slots.start // PER_COLUMN : slots.stop // PER_COLUMN]
-            nc.scalar.activation(picks[m][:, slots], o_tiles[m][:].indirect(entries), COPY)
+        def pick(m):
+            nc.scalar.activation(picks[m][:], o_tiles[m][:].indirect(offsets[:]), COPY)
 
         for h in range(2):
             for m in range(2):
@@ -149,25 +151,21 @@ def tile_attend_gdelta_kernel(tc, dyT, oT, wo_words, wo_scales, gq, offs, out_0,
         for h in range(2):
             place_by_scalar(0, h)
         store(0)
-        nc.vector.tensor_copy(windows[1][:].indirect(offsets[:]), grads[1][:])
+        place_by_vector(1)
         store(1)
-        pick(0, whole)
-        for m in range(SLABS - 1, 1, -1):
-            gated_product(m, whole, 2 + m)
-        pick(1, whole)
-        place_by_scalar(3, 0)
-        place_by_vector(3, 1)
-        store(3)
-        nc.vector.tensor_copy(windows[2][:].indirect(offsets[:]), grads[2][:])
-        store(2)
-        pick(2, whole)
-        pick(3, whole)
+        ungated = keep.tile([P, 2, SLOTS], F32, name="ungated")
+        for m in range(2, SLABS):
+            nc.scalar.copy(out=ungated[:, m - 2, :], in_=product(m, whole, 2 + m)[:])
+            nc.gpsimd.tensor_tensor(grads[m][:], ungated[:, m - 2, :], gate[:], MULT)
+            place_by_vector(m)
+            store(m)
+        for m in range(SLABS):
+            pick(m)
 
         sums = [psum.tile([P, P], F32, name="sum%d" % j, tag="bank%d" % j) for j in range(BLOCKS)]
         terms = [keep.tile([P, SLOTS], F32, name="term%d" % m) for m in range(SLABS)]
         for m in range(SLABS):
-            engine = nc.vector if m == SLABS - 1 else nc.gpsimd
-            engine.tensor_tensor(terms[m][:], picks[m][:], grads[m][:], MULT)
+            nc.gpsimd.tensor_tensor(terms[m][:], picks[m][:], grads[m][:], MULT)
             for j in range(BLOCKS):
                 nc.tensor.matmul(
                     sums[j][:],

@@ -40,13 +40,14 @@ def tile_attend_gdelta_kernel(tc, dyT, oT, wo_words, wo_scales, gq, offs, out_0,
         w_scales = keep.tile([P, E], U8, name="w_scales", align_bytes=64)
         nc.gpsimd.memset(w_scales[:].bitcast(I32), 0)
         gate_line = keep.tile([1, T], F32, name="gate_line", tag="line")
-        nc.sync.dma_start(out=gate_line[:], in_=gq[0:1, :])
-        nc.sync.dma_start(offsets[:], offs)
+        nc.scalar.dma_start(out=gate_line[:], in_=gq[0:1, :])
 
         dy_planes = [keep.tile([P, T], F32, name="dy%d" % t, tag="wide%d" % t) for t in range(PACK)]
         dy_rows = dyT.rearrange("(p t) w -> t p w", t=PACK)
         for t in range(PACK):
             nc.sync.dma_start(out=dy_planes[t][:], in_=dy_rows[t])
+            if t == 0:
+                nc.sync.dma_start(offsets[:], offs)
         w_words = keep.tile([P, E], U32, name="w_words", align_bytes=64)
         nc.sync.dma_start(out=w_words[:].bitcast(I32), in_=wo_words[0].rearrange("p n t -> p (n t)").bitcast(I32))
         for quad in range(P // QUAD):
@@ -178,12 +179,9 @@ def tile_attend_gdelta_kernel(tc, dyT, oT, wo_words, wo_scales, gq, offs, out_0,
 
         spent = keep.tile([P, BLOCKS, P], F32, name="spent")
         for j in range(BLOCKS):
-            nc.scalar.activation(
-                spent[:, j, :], sums[j][:], COPY, accum_out=delta_cols[:, QUAD * j : QUAD * j + 1]
-            )
-        delta_rows = keep.tile([P, P], F32, name="delta_rows", align_bytes=64)
-        nc.vector.transpose(delta_rows[:], delta_cols[:])
-        nc.scalar.dma_start(
-            out=out_1[0].rearrange("(j q r) -> q j r", j=BLOCKS, r=QUAD),
-            in_=delta_rows[0:P:QUAD, :].rearrange("q (j r) -> q j r", r=QUAD),
-        )
+            nc.scalar.activation(spent[:, j, :], sums[j][:], COPY, accum_out=delta_cols[:, j : j + 1])
+        delta_turned = psum.tile([P, P], F32, name="delta_turned", tag="bank4")
+        nc.tensor.transpose(delta_turned[:], delta_cols[:], ident[:])
+        delta_rows = keep.tile([BLOCKS, P], F32, name="delta_rows")
+        nc.scalar.copy(out=delta_rows[:], in_=delta_turned[0:BLOCKS, :])
+        nc.scalar.dma_start(out=out_1[0].rearrange("(j s) -> j s", j=BLOCKS), in_=delta_rows[:])

@@ -143,12 +143,8 @@ def tile_attend_gdelta_kernel(tc, dyT, oT, wo_words, wo_scales, gq, offs, out_0,
         def store(m):
             nc.sync.dma_start(out=out_0[m * P : (m + 1) * P, :], in_=windows[m][:])
 
-        def pick(m):
-            nc.scalar.activation(picks[m][:], o_tiles[m][:].indirect(offsets[:]), COPY)
-
-        for h in range(2):
-            for m in range(2):
-                gated_product(m, halves[h], 2 * h + m)
+        for bank, (m, h) in enumerate([(0, 0), (1, 0), (1, 1), (0, 1)]):
+            gated_product(m, halves[h], bank)
         for h in range(2):
             place_by_scalar(0, h)
         store(0)
@@ -160,22 +156,23 @@ def tile_attend_gdelta_kernel(tc, dyT, oT, wo_words, wo_scales, gq, offs, out_0,
             nc.gpsimd.tensor_tensor(grads[m][:], ungated[:, m - 2, :], gate[:], MULT)
             place_by_vector(m)
             store(m)
-        for m in range(SLABS):
-            pick(m)
 
         sums = [psum.tile([P, P], F32, name="sum%d" % j, tag="bank%d" % j) for j in range(BLOCKS)]
         terms = [keep.tile([P, SLOTS], F32, name="term%d" % m) for m in range(SLABS)]
         for m in range(SLABS):
-            nc.gpsimd.tensor_tensor(terms[m][:], picks[m][:], grads[m][:], MULT)
-            for j in range(BLOCKS):
-                nc.tensor.matmul(
-                    sums[j][:],
-                    lhsT=terms[m][:, j * P : (j + 1) * P],
-                    rhs=ident[:],
-                    is_transpose=True,
-                    start=m == 0,
-                    stop=m == SLABS - 1,
-                )
+            for slots in halves if m == SLABS - 1 else [whole]:
+                entries = offsets[:, slots.start // PER_COLUMN : slots.stop // PER_COLUMN]
+                nc.scalar.activation(picks[m][:, slots], o_tiles[m][:].indirect(entries), COPY)
+                nc.gpsimd.tensor_tensor(terms[m][:, slots], picks[m][:, slots], grads[m][:, slots], MULT)
+                for j in range(slots.start // P, slots.stop // P):
+                    nc.tensor.matmul(
+                        sums[j][:],
+                        lhsT=terms[m][:, j * P : (j + 1) * P],
+                        rhs=ident[:],
+                        is_transpose=True,
+                        start=m == 0,
+                        stop=m == SLABS - 1,
+                    )
 
         spent = keep.tile([P, BLOCKS, P], F32, name="spent")
         for j in range(BLOCKS):

@@ -31,6 +31,7 @@ def tile_attend_gdelta_kernel(tc, dyT, oT, wo_words, wo_scales, gq, offs, out_0,
     nc = tc.nc
     with ExitStack() as ctx:
         keep = ctx.enter_context(tc.tile_pool(name="keep", bufs=1))
+        wide = ctx.enter_context(tc.tile_pool(name="wide", bufs=1))
         psum = ctx.enter_context(tc.psum_pool(name="psum", bufs=1))
 
         offsets = keep.tile([P, SLOTS // PER_COLUMN], U16, name="offsets")
@@ -42,12 +43,13 @@ def tile_attend_gdelta_kernel(tc, dyT, oT, wo_words, wo_scales, gq, offs, out_0,
         gate_line = keep.tile([1, T], F32, name="gate_line", tag="line")
         nc.scalar.dma_start(out=gate_line[:], in_=gq[0:1, :])
 
-        dy_planes = [keep.tile([P, T], F32, name="dy%d" % t, tag="wide%d" % t) for t in range(PACK)]
-        dy_rows = dyT.rearrange("(p t) w -> t p w", t=PACK)
-        for t in range(PACK):
-            nc.sync.dma_start(out=dy_planes[t][:], in_=dy_rows[t])
-            if t == 0:
-                nc.sync.dma_start(offsets[:], offs)
+        dy_rows = dyT.rearrange("(p t) w -> p t w", t=PACK)
+        dy_pair = wide.tile([P, 2, T], F32, name="dy_pair", offset=4 * T)
+        dy_planes = {2: wide.tile([P, T], F32, name="dy2", offset=0), 3: wide.tile([P, T], F32, name="dy3", offset=12 * T)}
+        nc.sync.dma_start(out=dy_planes[2][:], in_=dy_rows[:, 2, :])
+        nc.sync.dma_start(offsets[:], offs)
+        nc.sync.dma_start(out=dy_pair[:], in_=dy_rows[:, 0:2, :])
+        nc.sync.dma_start(out=dy_planes[3][:], in_=dy_rows[:, 3, :])
         w_words = keep.tile([P, E], U32, name="w_words", align_bytes=64)
         nc.sync.dma_start(out=w_words[:].bitcast(I32), in_=wo_words[0].rearrange("p n t -> p (n t)").bitcast(I32))
         for quad in range(P // QUAD):
@@ -85,20 +87,21 @@ def tile_attend_gdelta_kernel(tc, dyT, oT, wo_words, wo_scales, gq, offs, out_0,
             nc.gpsimd.memset(windows[m][:].bitcast(I32), 0)
 
         grouped = [keep.tile([P, HALF, PACK], BF16, name="grouped%d" % h, tag="grouped%d" % h, align_bytes=64) for h in range(2)]
-        first_pair = keep.tile([P, 2, SLOTS], BF16, name="first_pair")
-        for t in range(2):
-            nc.vector.tensor_copy(first_pair[:, t, :], dy_planes[t][:].indirect(offsets[:]))
-        for h in range(2):
-            nc.scalar.copy(out=grouped[h][:, :, 0:2], in_=first_pair[:, :, halves[h]].rearrange("p t s -> p s t"))
-
         second_pair = keep.tile([P, 2, HALF], BF16, name="second_pair")
-        nc.vector.tensor_copy(second_pair[:, 0, :], dy_planes[2][:].indirect(half_lists[1]))
-        for t in range(2, PACK):
-            nc.vector.tensor_copy(grouped[0][:, :, t], dy_planes[t][:].indirect(half_lists[0]))
+        nc.scalar.activation(second_pair[:, 0, :], dy_planes[2][:].indirect(half_lists[1]), COPY)
+        nc.vector.tensor_copy(grouped[0][:, :, 2], dy_planes[2][:].indirect(half_lists[0]))
+
+        first_pair = keep.tile([P, 2, HALF], F32, name="first_pair")
+        for t in range(2):
+            nc.vector.tensor_copy(grouped[0][:, :, t], dy_pair[:, t, :].indirect(half_lists[0]))
+            nc.scalar.activation(first_pair[:, t, :], dy_pair[:, t, :].indirect(half_lists[1]), COPY)
+        nc.scalar.copy(out=grouped[1][:, :, 0:2], in_=first_pair[:].rearrange("p t s -> p s t"))
+
+        nc.vector.tensor_copy(grouped[0][:, :, 3], dy_planes[3][:].indirect(half_lists[0]))
         nc.scalar.activation(second_pair[:, 1, :], dy_planes[3][:].indirect(half_lists[1]), COPY)
         nc.vector.tensor_copy(out=grouped[1][:, :, 2:4], in_=second_pair[:].rearrange("p t s -> p s t"))
 
-        o_tiles = [keep.tile([P, T], F32, name="o%d" % m, tag="wide%d" % m) for m in range(SLABS)]
+        o_tiles = [wide.tile([P, T], F32, name="o%d" % m, offset=4 * T * m) for m in range(SLABS)]
         for m in range(SLABS):
             nc.sync.dma_start(out=o_tiles[m][:], in_=oT[m * P : (m + 1) * P, :])
 

@@ -144,7 +144,8 @@ def tile_attend_gdelta_kernel(tc, dyT, oT, wo_words, wo_scales, gq, offs, out_0,
             nc.vector.tensor_copy(windows[m][:].indirect(offsets[:]), grads[m][:])
 
         def store(m):
-            nc.sync.dma_start(out=out_0[m * P : (m + 1) * P, :], in_=windows[m][:])
+            for c in range(0, T, T // 2):
+                nc.sync.dma_start(out=out_0[m * P : (m + 1) * P, c : c + T // 2], in_=windows[m][:, c : c + T // 2])
 
         for bank, (m, h) in enumerate([(0, 0), (1, 0), (1, 1), (0, 1)]):
             gated_product(m, halves[h], bank)

@@ -11,6 +11,7 @@ BLOCKS = SLOTS // P
 QUAD = 32
 PER_COLUMN = 16
 HALF = SLOTS // 2
+ROW_BYTES = 4 * T
 
 FLOPS = 2 * D * E * SLOTS
 BYTES = 4 * (D * T + 2 * E * T + T + SLOTS) + D * E + D * E // 32 + 2 * P * SLOTS // 16
@@ -40,16 +41,16 @@ def tile_attend_gdelta_kernel(tc, dyT, oT, wo_words, wo_scales, gq, offs, out_0,
 
         w_scales = keep.tile([P, E], U8, name="w_scales", align_bytes=64)
         nc.gpsimd.memset(w_scales[:].bitcast(I32), 0)
-        gate_line = keep.tile([1, T], F32, name="gate_line", tag="line")
-        nc.scalar.dma_start(out=gate_line[:], in_=gq[0:1, :])
+        gate_table = keep.tile([P, T], F32, name="gate_table", tag="table")
+        nc.gpsimd.memset(gate_table[0 : P - 1, :].bitcast(I32), 0)
+        nc.scalar.dma_start(out=gate_table[P - 1 : P, :], in_=gq[0:1, :])
 
         dy_rows = dyT.rearrange("(p t) w -> p t w", t=PACK)
-        dy_pair = wide.tile([P, 2, T], F32, name="dy_pair", offset=4 * T)
-        dy_planes = {2: wide.tile([P, T], F32, name="dy2", offset=0), 3: wide.tile([P, T], F32, name="dy3", offset=12 * T)}
-        nc.sync.dma_start(out=dy_planes[2][:], in_=dy_rows[:, 2, :])
+        planes = [wide.tile([P, T], F32, name="dy%d" % t, offset=ROW_BYTES * t) for t in range(PACK)]
+        nc.sync.dma_start(out=planes[0][:], in_=dy_rows[:, 0, :])
         nc.sync.dma_start(offsets[:], offs)
-        nc.sync.dma_start(out=dy_pair[:], in_=dy_rows[:, 0:2, :])
-        nc.sync.dma_start(out=dy_planes[3][:], in_=dy_rows[:, 3, :])
+        for t in range(1, PACK):
+            nc.sync.dma_start(out=planes[t][:], in_=dy_rows[:, t, :])
         w_words = keep.tile([P, E], U32, name="w_words", align_bytes=64)
         nc.sync.dma_start(out=w_words[:].bitcast(I32), in_=wo_words[0].rearrange("p n t -> p (n t)").bitcast(I32))
         for quad in range(P // QUAD):
@@ -57,111 +58,94 @@ def tile_attend_gdelta_kernel(tc, dyT, oT, wo_words, wo_scales, gq, offs, out_0,
                 out=w_scales[QUAD * quad : QUAD * quad + 4, :].bitcast(I32),
                 in_=wo_scales[0, 4 * quad : 4 * quad + 4, :].bitcast(I32),
             )
-        gate_table = keep.tile([P, T], F32, name="gate_table", tag="table")
-        nc.gpsimd.memset(gate_table[:].bitcast(I32), 0)
-        nc.vector.tensor_copy(gate_table[0:1, :], gate_line[:])
 
         ident = keep.tile([P, P], F32, name="ident")
         make_identity(nc, ident[:])
         delta_cols = keep.tile([P, P], F32, name="delta_cols", align_bytes=64)
         nc.gpsimd.memset(delta_cols[:], 0.0)
+        windows = {}
+        for m in range(SLABS - 1):
+            windows[m] = keep.tile([P, T], F32, name="window%d" % m)
+            nc.gpsimd.memset(windows[m][:].bitcast(I32), 0)
 
-        windows = {0: keep.tile([P, T], F32, name="window0", tag="line")}
-        nc.gpsimd.memset(windows[0][:].bitcast(I32), 0)
-
-        gate_row = keep.tile([P, SLOTS], F32, name="gate_row", tag="row")
+        gate_row = keep.tile([P, SLOTS], F32, name="gate_row")
         nc.vector.tensor_copy(gate_row[:], gate_table[:].indirect(offsets[:]))
         gate_turned = psum.tile([P, BLOCKS, P], F32, name="gate_turned", tag="bank6")
         for j in range(BLOCKS):
             nc.tensor.transpose(gate_turned[:, j, :], gate_row[:, j * P : (j + 1) * P], ident[:])
         gate_cols = keep.tile([P, BLOCKS], F32, name="gate_cols")
-        nc.scalar.activation(gate_cols[:], gate_turned[:, :, 0], COPY)
+        nc.scalar.activation(gate_cols[:], gate_turned[:, :, P - 1], COPY)
         gate_spread = psum.tile([P, BLOCKS, P], F32, name="gate_spread", tag="bank7")
         for j in range(BLOCKS):
             nc.tensor.transpose(gate_spread[:, j, :], gate_cols[:, j : j + 1].to_broadcast([P, P]), ident[:])
         gate = keep.tile([P, SLOTS], F32, name="gate")
         nc.scalar.copy(out=gate[:], in_=gate_spread[:].rearrange("p j s -> p (j s)"))
-        windows[1] = keep.tile([P, T], F32, name="window1", tag="table")
-        windows[2] = keep.tile([P, T], F32, name="window2", tag="row")
-        for m in (1, 2):
-            nc.gpsimd.memset(windows[m][:].bitcast(I32), 0)
 
         grouped = [keep.tile([P, HALF, PACK], BF16, name="grouped%d" % h, tag="grouped%d" % h, align_bytes=64) for h in range(2)]
-        second_pair = keep.tile([P, 2, HALF], BF16, name="second_pair")
-        nc.scalar.activation(second_pair[:, 0, :], dy_planes[2][:].indirect(half_lists[1]), COPY)
-        nc.vector.tensor_copy(grouped[0][:, :, 2], dy_planes[2][:].indirect(half_lists[0]))
+        for t in range(PACK):
+            nc.vector.tensor_copy(grouped[0][:, :, t], planes[t][:].indirect(half_lists[0]))
+            nc.scalar.activation(grouped[1][:, :, t], planes[t][:].indirect(half_lists[1]), COPY)
 
-        first_pair = keep.tile([P, 2, HALF], F32, name="first_pair")
-        for t in range(2):
-            nc.vector.tensor_copy(grouped[0][:, :, t], dy_pair[:, t, :].indirect(half_lists[0]))
-            nc.scalar.activation(first_pair[:, t, :], dy_pair[:, t, :].indirect(half_lists[1]), COPY)
-        nc.scalar.copy(out=grouped[1][:, :, 0:2], in_=first_pair[:].rearrange("p t s -> p s t"))
-
-        nc.vector.tensor_copy(grouped[0][:, :, 3], dy_planes[3][:].indirect(half_lists[0]))
-        nc.scalar.activation(second_pair[:, 1, :], dy_planes[3][:].indirect(half_lists[1]), COPY)
-        nc.vector.tensor_copy(out=grouped[1][:, :, 2:4], in_=second_pair[:].rearrange("p t s -> p s t"))
-
-        o_tiles = [wide.tile([P, T], F32, name="o%d" % m, offset=4 * T * m) for m in range(SLABS)]
-        for m in range(SLABS):
-            nc.sync.dma_start(out=o_tiles[m][:], in_=oT[m * P : (m + 1) * P, :])
-
-        dy_words = keep.tile([P, SLOTS], U32, name="dy_words", align_bytes=64)
-        dy_scales = keep.tile([P, SLOTS], U8, name="dy_scales", align_bytes=64)
-        for h in range(2):
+        last_plane = ROW_BYTES * (PACK - 1)
+        dy_words = [
+            wide.tile([P, HALF], U32, name="dy_words0", offset=last_plane, align_bytes=64),
+            keep.tile([P, HALF], U32, name="dy_words1", align_bytes=64),
+        ]
+        dy_scales = [keep.tile([P, HALF], U8, name="dy_scales%d" % h, align_bytes=64) for h in range(2)]
+        for h in (1, 0):
             nc.vector.quantize_mx(
-                out=dy_words[:, halves[h]].bitcast(E5M2),
-                scales=dy_scales[:, halves[h]],
+                out=dy_words[h][:].bitcast(E5M2),
+                scales=dy_scales[h][:],
                 in_=grouped[h][:].rearrange("p s t -> p (s t)"),
             )
 
-        windows[3] = keep.tile([P, T], F32, name="window3", tag="grouped1", align_bytes=64)
+        o_offsets = [ROW_BYTES * m for m in range(SLABS - 1)] + [last_plane + 4 * HALF]
+        o_tiles = [wide.tile([P, T], F32, name="o%d" % m, offset=o_offsets[m]) for m in range(SLABS)]
+        for m in range(SLABS):
+            nc.sync.dma_start(out=o_tiles[m][:], in_=oT[m * P : (m + 1) * P, :])
+
+        windows[3] = keep.tile([P, T], F32, name="window3", tag="grouped0", align_bytes=64)
         nc.gpsimd.memset(windows[3][:].bitcast(I32), 0)
 
         grads = [keep.tile([P, SLOTS], F32, name="grad%d" % m) for m in range(SLABS)]
         picks = [keep.tile([P, SLOTS], F32, name="pick%d" % m) for m in range(SLABS)]
         whole = slice(0, SLOTS)
 
-        def product(m, slots, bank):
-            prod = psum.tile([P, slots.stop - slots.start], F32, name="prod", tag="bank%d" % bank)
+        def product(m, h, out):
             nc.tensor.matmul_mx(
-                out=prod[:],
+                out=out,
                 lhsT=w_words[:, m * P : (m + 1) * P].bitcast(E4M3),
                 lhsT_scale=w_scales[:, m * P : (m + 1) * P],
-                rhs=dy_words[:, slots].bitcast(E5M2),
-                rhs_scale=dy_scales[:, slots],
+                rhs=dy_words[h][:].bitcast(E5M2),
+                rhs_scale=dy_scales[h][:],
                 start=True,
                 stop=True,
             )
-            return prod
-
-        def gated_product(m, slots, bank):
-            nc.vector.tensor_tensor(grads[m][:, slots], product(m, slots, bank)[:], gate[:, slots], MULT)
-
-        def place_by_scalar(m, h):
-            nc.scalar.activation(windows[m][:].indirect(half_lists[h]), grads[m][:, halves[h]], COPY)
-
-        def place_by_vector(m):
-            nc.vector.tensor_copy(windows[m][:].indirect(offsets[:]), grads[m][:])
 
         def store(m):
             for c in range(0, T, T // 2):
                 nc.sync.dma_start(out=out_0[m * P : (m + 1) * P, c : c + T // 2], in_=windows[m][:, c : c + T // 2])
 
-        for bank, (m, h) in enumerate([(0, 0), (1, 0), (1, 1), (0, 1)]):
-            gated_product(m, halves[h], bank)
-        for h in range(2):
-            place_by_scalar(0, h)
+        for bank, (m, h) in enumerate([(0, 1), (1, 1), (1, 0), (0, 0)]):
+            prod = psum.tile([P, HALF], F32, name="prod", tag="bank%d" % bank)
+            product(m, h, prod[:])
+            nc.vector.tensor_tensor(grads[m][:, halves[h]], prod[:], gate[:, halves[h]], MULT)
+        for h in (1, 0):
+            nc.scalar.activation(windows[0][:].indirect(half_lists[h]), grads[0][:, halves[h]], COPY)
         store(0)
-        place_by_vector(1)
+        nc.vector.tensor_copy(windows[1][:].indirect(offsets[:]), grads[1][:])
         store(1)
         ungated = keep.tile([P, 2, SLOTS], F32, name="ungated")
         for m in range(2, SLABS):
-            nc.scalar.copy(out=ungated[:, m - 2, :], in_=product(m, whole, 2 + m)[:])
+            prod = psum.tile([P, SLOTS], F32, name="prod", tag="bank%d" % (m - 2))
+            for h in (1, 0):
+                product(m, h, prod[:, halves[h]])
+            nc.scalar.copy(out=ungated[:, m - 2, :], in_=prod[:])
             nc.gpsimd.tensor_tensor(grads[m][:], ungated[:, m - 2, :], gate[:], MULT)
-            place_by_vector(m)
+            nc.vector.tensor_copy(windows[m][:].indirect(offsets[:]), grads[m][:])
             store(m)
 
-        sums = [psum.tile([P, P], F32, name="sum%d" % j, tag="bank%d" % j) for j in range(BLOCKS)]
+        sums = [psum.tile([P, P], F32, name="sum%d" % j, tag="bank%d" % (4 + j)) for j in range(BLOCKS)]
         terms = [keep.tile([P, SLOTS], F32, name="term%d" % m) for m in range(SLABS)]
         for m in range(SLABS):
             for slots in halves if m == SLABS - 1 else [whole]:
@@ -181,7 +165,7 @@ def tile_attend_gdelta_kernel(tc, dyT, oT, wo_words, wo_scales, gq, offs, out_0,
         spent = keep.tile([P, BLOCKS, P], F32, name="spent")
         for j in range(BLOCKS):
             nc.scalar.activation(spent[:, j, :], sums[j][:], COPY, accum_out=delta_cols[:, j : j + 1])
-        delta_turned = psum.tile([P, P], F32, name="delta_turned", tag="bank4")
+        delta_turned = psum.tile([P, P], F32, name="delta_turned", tag="bank2")
         nc.tensor.transpose(delta_turned[:], delta_cols[:], ident[:])
         delta_rows = keep.tile([BLOCKS, P], F32, name="delta_rows")
         nc.scalar.copy(out=delta_rows[:], in_=delta_turned[0:BLOCKS, :])

@@ -12,6 +12,7 @@ QUAD = 32
 PER_COLUMN = 16
 HALF = SLOTS // 2
 ROW_BYTES = 4 * T
+STEP = QUAD // BLOCKS
 
 FLOPS = 2 * D * E * SLOTS
 BYTES = 4 * (D * T + 2 * E * T + T + SLOTS) + D * E + D * E // 32 + 2 * P * SLOTS // 16
@@ -25,6 +26,7 @@ U8 = mybir.dt.uint8
 E4M3 = mybir.dt.float8_e4m3fn_x4
 E5M2 = mybir.dt.float8_e5m2_x4
 MULT = mybir.AluOpType.mult
+ADD = mybir.AluOpType.add
 COPY = mybir.ActivationFunctionType.Copy
 
 
@@ -41,7 +43,7 @@ def tile_attend_gdelta_kernel(tc, dyT, oT, wo_words, wo_scales, gq, offs, out_0,
 
         w_scales = keep.tile([P, E], U8, name="w_scales", align_bytes=64)
         nc.gpsimd.memset(w_scales[:].bitcast(I32), 0)
-        gate_table = keep.tile([P, T], F32, name="gate_table", tag="table")
+        gate_table = keep.tile([P, T], F32, name="gate_table", tag="grouped0", align_bytes=64)
         nc.gpsimd.memset(gate_table[0 : P - 1, :].bitcast(I32), 0)
         nc.scalar.dma_start(out=gate_table[P - 1 : P, :], in_=gq[0:1, :])
 
@@ -61,14 +63,14 @@ def tile_attend_gdelta_kernel(tc, dyT, oT, wo_words, wo_scales, gq, offs, out_0,
 
         ident = keep.tile([P, P], F32, name="ident")
         make_identity(nc, ident[:])
-        delta_cols = keep.tile([P, P], F32, name="delta_cols", align_bytes=64)
+        delta_cols = keep.tile([P, QUAD], F32, name="delta_cols", align_bytes=64)
         nc.gpsimd.memset(delta_cols[:], 0.0)
         windows = {}
         for m in range(SLABS - 1):
             windows[m] = keep.tile([P, T], F32, name="window%d" % m)
             nc.gpsimd.memset(windows[m][:].bitcast(I32), 0)
 
-        gate_row = keep.tile([P, SLOTS], F32, name="gate_row")
+        gate_row = keep.tile([P, SLOTS], F32, name="gate_row", tag="grouped1", align_bytes=64)
         nc.vector.tensor_copy(gate_row[:], gate_table[:].indirect(offsets[:]))
         gate_turned = psum.tile([P, BLOCKS, P], F32, name="gate_turned", tag="bank6")
         for j in range(BLOCKS):
@@ -109,7 +111,6 @@ def tile_attend_gdelta_kernel(tc, dyT, oT, wo_words, wo_scales, gq, offs, out_0,
 
         grads = [keep.tile([P, SLOTS], F32, name="grad%d" % m) for m in range(SLABS)]
         picks = [keep.tile([P, SLOTS], F32, name="pick%d" % m) for m in range(SLABS)]
-        whole = slice(0, SLOTS)
 
         def product(m, h, out):
             nc.tensor.matmul_mx(
@@ -126,47 +127,62 @@ def tile_attend_gdelta_kernel(tc, dyT, oT, wo_words, wo_scales, gq, offs, out_0,
             for c in range(0, T, T // 2):
                 nc.sync.dma_start(out=out_0[m * P : (m + 1) * P, c : c + T // 2], in_=windows[m][:, c : c + T // 2])
 
-        for bank, (m, h) in enumerate([(0, 1), (1, 1), (1, 0), (0, 0)]):
+        def banked_product(m, h, bank):
             prod = psum.tile([P, HALF], F32, name="prod", tag="bank%d" % bank)
             product(m, h, prod[:])
-            nc.vector.tensor_tensor(grads[m][:, halves[h]], prod[:], gate[:, halves[h]], MULT)
-        for h in (1, 0):
-            nc.scalar.activation(windows[0][:].indirect(half_lists[h]), grads[0][:, halves[h]], COPY)
-        store(0)
-        nc.vector.tensor_copy(windows[1][:].indirect(offsets[:]), grads[1][:])
-        store(1)
-        ungated = keep.tile([P, 2, SLOTS], F32, name="ungated")
-        for m in range(2, SLABS):
-            prod = psum.tile([P, SLOTS], F32, name="prod", tag="bank%d" % (m - 2))
-            for h in (1, 0):
-                product(m, h, prod[:, halves[h]])
-            nc.scalar.copy(out=ungated[:, m - 2, :], in_=prod[:])
-            nc.gpsimd.tensor_tensor(grads[m][:], ungated[:, m - 2, :], gate[:], MULT)
-            nc.vector.tensor_copy(windows[m][:].indirect(offsets[:]), grads[m][:])
-            store(m)
+            return prod
 
-        sums = [psum.tile([P, P], F32, name="sum%d" % j, tag="bank%d" % (4 + j)) for j in range(BLOCKS)]
+        def gate_on_vector(m, h, bank):
+            nc.vector.tensor_tensor(grads[m][:, halves[h]], banked_product(m, h, bank)[:], gate[:, halves[h]], MULT)
+
+        def place_by_scalar(m, h):
+            nc.scalar.activation(windows[m][:].indirect(half_lists[h]), grads[m][:, halves[h]], COPY)
+
+        def place_by_vector(m, slots, entries):
+            nc.vector.tensor_copy(windows[m][:].indirect(entries), grads[m][:, slots])
+
+        for bank, (m, h) in zip((0, 1, 2, 0, 3), [(0, 1), (1, 1), (1, 0), (3, 1), (0, 0)]):
+            gate_on_vector(m, h, bank)
+        for m, h in [(0, 1), (3, 1), (0, 0)]:
+            place_by_scalar(m, h)
+        place_by_vector(1, slice(0, SLOTS), offsets[:])
+        store(1)
+        store(0)
+        prod = psum.tile([P, SLOTS], F32, name="prod", tag="bank1")
+        for h in (1, 0):
+            product(2, h, prod[:, halves[h]])
+        nc.vector.tensor_tensor(grads[2][:], prod[:], gate[:], MULT)
+        gate_on_vector(3, 0, 2)
+        place_by_vector(2, slice(0, SLOTS), offsets[:])
+        store(2)
+        place_by_vector(3, halves[0], half_lists[0])
+        store(3)
+
+        sums = [psum.tile([P, P], F32, name="sum%d" % j, tag="bank%d" % bank) for j, bank in enumerate((4, 5, 6, 7))]
         terms = [keep.tile([P, SLOTS], F32, name="term%d" % m) for m in range(SLABS)]
         for m in range(SLABS):
-            for slots in halves if m == SLABS - 1 else [whole]:
-                entries = offsets[:, slots.start // PER_COLUMN : slots.stop // PER_COLUMN]
-                nc.scalar.activation(picks[m][:, slots], o_tiles[m][:].indirect(entries), COPY)
-                nc.gpsimd.tensor_tensor(terms[m][:, slots], picks[m][:, slots], grads[m][:, slots], MULT)
-                for j in range(slots.start // P, slots.stop // P):
+            last = m == SLABS - 1
+            for h in range(2):
+                nc.scalar.activation(picks[m][:, halves[h]], o_tiles[m][:].indirect(half_lists[h]), COPY)
+                engine = nc.vector if last else nc.gpsimd
+                engine.tensor_tensor(terms[m][:, halves[h]], picks[m][:, halves[h]], grads[m][:, halves[h]], MULT)
+                for j in range(2 * h, 2 * h + 2):
                     nc.tensor.matmul(
                         sums[j][:],
                         lhsT=terms[m][:, j * P : (j + 1) * P],
                         rhs=ident[:],
                         is_transpose=True,
                         start=m == 0,
-                        stop=m == SLABS - 1,
+                        stop=last,
                     )
 
-        spent = keep.tile([P, BLOCKS, P], F32, name="spent")
+        spent = keep.tile([P, BLOCKS // 2, P], F32, name="spent")
         for j in range(BLOCKS):
-            nc.scalar.activation(spent[:, j, :], sums[j][:], COPY, accum_out=delta_cols[:, j : j + 1])
-        delta_turned = psum.tile([P, P], F32, name="delta_turned", tag="bank2")
-        nc.tensor.transpose(delta_turned[:], delta_cols[:], ident[:])
-        delta_rows = keep.tile([BLOCKS, P], F32, name="delta_rows")
-        nc.scalar.copy(out=delta_rows[:], in_=delta_turned[0:BLOCKS, :])
-        nc.scalar.dma_start(out=out_1[0].rearrange("(j s) -> j s", j=BLOCKS), in_=delta_rows[:])
+            column = delta_cols[:, STEP * j : STEP * j + 1]
+            if j % 2 == 0:
+                nc.scalar.activation(spent[:, j // 2, :], sums[j][:], COPY, accum_out=column)
+            else:
+                nc.vector.tensor_reduce(out=column, in_=sums[j][:], op=ADD, axis=mybir.AxisListType.X)
+        delta_rows = keep.tile([P, QUAD], F32, name="delta_rows", align_bytes=64)
+        nc.vector.transpose(delta_rows[:], delta_cols[:])
+        nc.scalar.dma_start(out=out_1[0].rearrange("(j q s) -> q j s", j=BLOCKS, q=P // QUAD), in_=delta_rows[0:P:STEP, :])

@@ -160,13 +160,15 @@ def tile_attend_gdelta_kernel(tc, dyT, oT, wo_words, wo_scales, gq, offs, out_0,
 
         sums = [psum.tile([P, P], F32, name="sum%d" % j, tag="bank%d" % bank) for j, bank in enumerate((4, 5, 6, 7))]
         terms = [keep.tile([P, SLOTS], F32, name="term%d" % m) for m in range(SLABS)]
+        last_pieces = [halves[0], slice(HALF, HALF + P), slice(HALF + P, SLOTS)]
         for m in range(SLABS):
             last = m == SLABS - 1
-            for h in range(2):
-                nc.scalar.activation(picks[m][:, halves[h]], o_tiles[m][:].indirect(half_lists[h]), COPY)
+            for slots in last_pieces if last else halves:
+                entries = offsets[:, slots.start // PER_COLUMN : slots.stop // PER_COLUMN]
+                nc.scalar.activation(picks[m][:, slots], o_tiles[m][:].indirect(entries), COPY)
                 engine = nc.vector if last else nc.gpsimd
-                engine.tensor_tensor(terms[m][:, halves[h]], picks[m][:, halves[h]], grads[m][:, halves[h]], MULT)
-                for j in range(2 * h, 2 * h + 2):
+                engine.tensor_tensor(terms[m][:, slots], picks[m][:, slots], grads[m][:, slots], MULT)
+                for j in range(slots.start // P, slots.stop // P):
                     nc.tensor.matmul(
                         sums[j][:],
                         lhsT=terms[m][:, j * P : (j + 1) * P],
@@ -176,11 +178,11 @@ def tile_attend_gdelta_kernel(tc, dyT, oT, wo_words, wo_scales, gq, offs, out_0,
                         stop=last,
                     )
 
-        spent = keep.tile([P, BLOCKS // 2, P], F32, name="spent")
+        spent = keep.tile([P, 2, P], F32, name="spent")
         for j in range(BLOCKS):
             column = delta_cols[:, STEP * j : STEP * j + 1]
-            if j % 2 == 0:
-                nc.scalar.activation(spent[:, j // 2, :], sums[j][:], COPY, accum_out=column)
+            if j in (0, BLOCKS - 1):
+                nc.scalar.activation(spent[:, j % 2, :], sums[j][:], COPY, accum_out=column)
             else:
                 nc.vector.tensor_reduce(out=column, in_=sums[j][:], op=ADD, axis=mybir.AxisListType.X)
         delta_rows = keep.tile([P, QUAD], F32, name="delta_rows", align_bytes=64)

@@ -80,7 +80,7 @@ def tile_attend_gdelta_kernel(tc, dyT, oT, wo_words, wo_scales, gq, offs, out_0,
         gate_spread = psum.tile([P, BLOCKS, P], F32, name="gate_spread", tag="bank7")
         for j in range(BLOCKS):
             nc.tensor.transpose(gate_spread[:, j, :], gate_cols[:, j : j + 1].to_broadcast([P, P]), ident[:])
-        gate = keep.tile([P, SLOTS], F32, name="gate")
+        gate = keep.tile([P, SLOTS], F32, name="gate", tag="gate")
         nc.scalar.copy(out=gate[:], in_=gate_spread[:].rearrange("p j s -> p (j s)"))
 
         grouped = [keep.tile([P, HALF, PACK], BF16, name="grouped%d" % h, tag="grouped%d" % h, align_bytes=64) for h in range(2)]
@@ -110,7 +110,6 @@ def tile_attend_gdelta_kernel(tc, dyT, oT, wo_words, wo_scales, gq, offs, out_0,
         nc.gpsimd.memset(windows[3][:].bitcast(I32), 0)
 
         grads = [keep.tile([P, SLOTS], F32, name="grad%d" % m) for m in range(SLABS)]
-        picks = [keep.tile([P, SLOTS], F32, name="pick%d" % m) for m in range(SLABS)]
 
         def product(m, h, out):
             nc.tensor.matmul_mx(
@@ -141,23 +140,25 @@ def tile_attend_gdelta_kernel(tc, dyT, oT, wo_words, wo_scales, gq, offs, out_0,
         def place_by_vector(m, slots, entries):
             nc.vector.tensor_copy(windows[m][:].indirect(entries), grads[m][:, slots])
 
-        for bank, (m, h) in zip((0, 1, 2, 0, 3), [(0, 1), (1, 1), (1, 0), (3, 1), (0, 0)]):
+        for bank, (m, h) in enumerate([(0, 1), (1, 1), (1, 0), (0, 0)]):
             gate_on_vector(m, h, bank)
-        for m, h in [(0, 1), (3, 1), (0, 0)]:
-            place_by_scalar(m, h)
-        place_by_vector(1, slice(0, SLOTS), offsets[:])
-        store(1)
-        store(0)
-        prod = psum.tile([P, SLOTS], F32, name="prod", tag="bank1")
+        prod = psum.tile([P, SLOTS], F32, name="prod", tag="bank0")
         for h in (1, 0):
             product(2, h, prod[:, halves[h]])
         nc.vector.tensor_tensor(grads[2][:], prod[:], gate[:], MULT)
+        gate_on_vector(3, 1, 1)
+        place_by_vector(2, halves[0], half_lists[0])
         gate_on_vector(3, 0, 2)
-        place_by_vector(2, slice(0, SLOTS), offsets[:])
+        for h in (1, 0):
+            place_by_scalar(0, h)
+        store(0)
+        place_by_scalar(2, 1)
         store(2)
-        place_by_vector(3, halves[0], half_lists[0])
-        store(3)
+        for m in (1, 3):
+            place_by_vector(m, slice(0, SLOTS), offsets[:])
+            store(m)
 
+        picks = [keep.tile([P, SLOTS], F32, name="pick%d" % m, tag="gate" if m == 0 else "pick%d" % m) for m in range(SLABS)]
         sums = [psum.tile([P, P], F32, name="sum%d" % j, tag="bank%d" % bank) for j, bank in enumerate((4, 5, 6, 7))]
         terms = [keep.tile([P, SLOTS], F32, name="term%d" % m) for m in range(SLABS)]
         last_pieces = [halves[0], slice(HALF, HALF + P), slice(HALF + P, SLOTS)]

@@ -13,6 +13,7 @@ PER_COLUMN = 16
 HALF = SLOTS // 2
 ROW_BYTES = 4 * T
 STEP = QUAD // BLOCKS
+FIRST_ON_VECTOR = 2 * SLOTS + HALF
 
 FLOPS = 2 * D * E * SLOTS
 BYTES = 4 * (D * T + 2 * E * T + T + SLOTS) + D * E + D * E // 32 + 2 * P * SLOTS // 16
@@ -80,7 +81,7 @@ def tile_attend_gdelta_kernel(tc, dyT, oT, wo_words, wo_scales, gq, offs, out_0,
         gate_spread = psum.tile([P, BLOCKS, P], F32, name="gate_spread", tag="bank7")
         for j in range(BLOCKS):
             nc.tensor.transpose(gate_spread[:, j, :], gate_cols[:, j : j + 1].to_broadcast([P, P]), ident[:])
-        gate = keep.tile([P, SLOTS], F32, name="gate", tag="gate")
+        gate = keep.tile([P, SLOTS], F32, name="gate")
         nc.scalar.copy(out=gate[:], in_=gate_spread[:].rearrange("p j s -> p (j s)"))
 
         grouped = [keep.tile([P, HALF, PACK], BF16, name="grouped%d" % h, tag="grouped%d" % h, align_bytes=64) for h in range(2)]
@@ -140,17 +141,20 @@ def tile_attend_gdelta_kernel(tc, dyT, oT, wo_words, wo_scales, gq, offs, out_0,
         def place_by_vector(m, slots, entries):
             nc.vector.tensor_copy(windows[m][:].indirect(entries), grads[m][:, slots])
 
-        for bank, (m, h) in enumerate([(0, 1), (1, 1), (1, 0), (0, 0)]):
+        for bank, (m, h) in enumerate([(0, 1), (1, 1), (1, 0)]):
             gate_on_vector(m, h, bank)
-        prod = psum.tile([P, SLOTS], F32, name="prod", tag="bank0")
+        place_by_scalar(0, 1)
+        prod = psum.tile([P, SLOTS], F32, name="prod", tag="bank3")
         for h in (1, 0):
             product(2, h, prod[:, halves[h]])
         nc.vector.tensor_tensor(grads[2][:], prod[:], gate[:], MULT)
-        gate_on_vector(3, 1, 1)
+        gate_on_vector(3, 1, 0)
+        ungated = keep.tile([P, HALF], F32, name="ungated")
+        nc.scalar.copy(out=ungated[:], in_=banked_product(3, 0, 1)[:])
+        nc.gpsimd.tensor_tensor(grads[3][:, halves[0]], ungated[:], gate[:, halves[0]], MULT)
+        gate_on_vector(0, 0, 2)
         place_by_vector(2, halves[0], half_lists[0])
-        gate_on_vector(3, 0, 2)
-        for h in (1, 0):
-            place_by_scalar(0, h)
+        place_by_scalar(0, 0)
         store(0)
         place_by_scalar(2, 1)
         store(2)
@@ -158,7 +162,7 @@ def tile_attend_gdelta_kernel(tc, dyT, oT, wo_words, wo_scales, gq, offs, out_0,
             place_by_vector(m, slice(0, SLOTS), offsets[:])
             store(m)
 
-        picks = [keep.tile([P, SLOTS], F32, name="pick%d" % m, tag="gate" if m == 0 else "pick%d" % m) for m in range(SLABS)]
+        picks = [keep.tile([P, SLOTS], F32, name="pick%d" % m) for m in range(SLABS)]
         sums = [psum.tile([P, P], F32, name="sum%d" % j, tag="bank%d" % bank) for j, bank in enumerate((4, 5, 6, 7))]
         terms = [keep.tile([P, SLOTS], F32, name="term%d" % m) for m in range(SLABS)]
         last_pieces = [halves[0], slice(HALF, HALF + P), slice(HALF + P, SLOTS)]
@@ -167,7 +171,7 @@ def tile_attend_gdelta_kernel(tc, dyT, oT, wo_words, wo_scales, gq, offs, out_0,
             for slots in last_pieces if last else halves:
                 entries = offsets[:, slots.start // PER_COLUMN : slots.stop // PER_COLUMN]
                 nc.scalar.activation(picks[m][:, slots], o_tiles[m][:].indirect(entries), COPY)
-                engine = nc.vector if last else nc.gpsimd
+                engine = nc.vector if m * SLOTS + slots.start >= FIRST_ON_VECTOR else nc.gpsimd
                 engine.tensor_tensor(terms[m][:, slots], picks[m][:, slots], grads[m][:, slots], MULT)
                 for j in range(slots.start // P, slots.stop // P):
                     nc.tensor.matmul(

@@ -12,6 +12,7 @@ QUAD = 32
 PER_COLUMN = 16
 HALF = SLOTS // 2
 ROW_BYTES = 4 * T
+WORD_BYTES = 4 * HALF
 STEP = QUAD // BLOCKS
 FIRST_ON_VECTOR = 2 * SLOTS + HALF
 
@@ -49,7 +50,7 @@ def tile_attend_gdelta_kernel(tc, dyT, oT, wo_words, wo_scales, gq, offs, out_0,
         nc.scalar.dma_start(out=gate_table[P - 1 : P, :], in_=gq[0:1, :])
 
         dy_rows = dyT.rearrange("(p t) w -> p t w", t=PACK)
-        planes = [wide.tile([P, T], F32, name="dy%d" % t, offset=ROW_BYTES * t) for t in range(PACK)]
+        planes = [wide.tile([P, T], F32, name="dy%d" % t, offset=WORD_BYTES + ROW_BYTES * t) for t in range(PACK)]
         nc.sync.dma_start(out=planes[0][:], in_=dy_rows[:, 0, :])
         nc.sync.dma_start(offsets[:], offs)
         for t in range(1, PACK):
@@ -89,9 +90,8 @@ def tile_attend_gdelta_kernel(tc, dyT, oT, wo_words, wo_scales, gq, offs, out_0,
             nc.vector.tensor_copy(grouped[0][:, :, t], planes[t][:].indirect(half_lists[0]))
             nc.scalar.activation(grouped[1][:, :, t], planes[t][:].indirect(half_lists[1]), COPY)
 
-        last_plane = ROW_BYTES * (PACK - 1)
         dy_words = [
-            wide.tile([P, HALF], U32, name="dy_words0", offset=last_plane, align_bytes=64),
+            wide.tile([P, HALF], U32, name="dy_words0", offset=ROW_BYTES * PACK, align_bytes=64),
             keep.tile([P, HALF], U32, name="dy_words1", align_bytes=64),
         ]
         dy_scales = [keep.tile([P, HALF], U8, name="dy_scales%d" % h, align_bytes=64) for h in range(2)]
@@ -102,10 +102,10 @@ def tile_attend_gdelta_kernel(tc, dyT, oT, wo_words, wo_scales, gq, offs, out_0,
                 in_=grouped[h][:].rearrange("p s t -> p (s t)"),
             )
 
-        o_offsets = [ROW_BYTES * m for m in range(SLABS - 1)] + [last_plane + 4 * HALF]
-        o_tiles = [wide.tile([P, T], F32, name="o%d" % m, offset=o_offsets[m]) for m in range(SLABS)]
-        for m in range(SLABS):
-            nc.sync.dma_start(out=o_tiles[m][:], in_=oT[m * P : (m + 1) * P, :])
+        o_rows = oT.rearrange("(m p) w -> p m w", p=P)
+        o_pairs = [wide.tile([P, 2, T], F32, name="o_pair%d" % u, offset=2 * ROW_BYTES * u) for u in range(SLABS // 2)]
+        for u in range(SLABS // 2):
+            nc.sync.dma_start(out=o_pairs[u][:], in_=o_rows[:, 2 * u : 2 * u + 2, :])
 
         windows[3] = keep.tile([P, T], F32, name="window3", tag="grouped0", align_bytes=64)
         nc.gpsimd.memset(windows[3][:].bitcast(I32), 0)
@@ -124,8 +124,7 @@ def tile_attend_gdelta_kernel(tc, dyT, oT, wo_words, wo_scales, gq, offs, out_0,
             )
 
         def store(m):
-            for c in range(0, T, T // 2):
-                nc.sync.dma_start(out=out_0[m * P : (m + 1) * P, c : c + T // 2], in_=windows[m][:, c : c + T // 2])
+            nc.sync.dma_start(out=out_0[m * P : (m + 1) * P, :], in_=windows[m][:])
 
         def banked_product(m, h, bank):
             prod = psum.tile([P, HALF], F32, name="prod", tag="bank%d" % bank)
@@ -170,7 +169,7 @@ def tile_attend_gdelta_kernel(tc, dyT, oT, wo_words, wo_scales, gq, offs, out_0,
             last = m == SLABS - 1
             for slots in last_pieces if last else halves:
                 entries = offsets[:, slots.start // PER_COLUMN : slots.stop // PER_COLUMN]
-                nc.scalar.activation(picks[m][:, slots], o_tiles[m][:].indirect(entries), COPY)
+                nc.scalar.activation(picks[m][:, slots], o_pairs[m // 2][:, m % 2, :].indirect(entries), COPY)
                 engine = nc.vector if m * SLOTS + slots.start >= FIRST_ON_VECTOR else nc.gpsimd
                 engine.tensor_tensor(terms[m][:, slots], picks[m][:, slots], grads[m][:, slots], MULT)
                 for j in range(slots.start // P, slots.stop // P):

from contextlib import ExitStack

import concourse.mybir as mybir
from concourse.masks import make_identity

D, E, SLOTS, T = 512, 512, 512, 2048
P = 128
PACK = 4
SLABS = E // P
BLOCKS = SLOTS // P
QUAD = 32
PER_COLUMN = 16
HALF = SLOTS // 2
ROW_BYTES = 4 * T
WORD_BYTES = 4 * HALF
STEP = QUAD // BLOCKS
FIRST_ON_VECTOR = 2 * SLOTS + HALF

FLOPS = 2 * D * E * SLOTS
BYTES = 4 * (D * T + 2 * E * T + T + SLOTS) + D * E + D * E // 32 + 2 * P * SLOTS // 16

F32 = mybir.dt.float32
BF16 = mybir.dt.bfloat16
I32 = mybir.dt.int32
U32 = mybir.dt.uint32
U16 = mybir.dt.uint16
U8 = mybir.dt.uint8
E4M3 = mybir.dt.float8_e4m3fn_x4
E5M2 = mybir.dt.float8_e5m2_x4
MULT = mybir.AluOpType.mult
ADD = mybir.AluOpType.add
COPY = mybir.ActivationFunctionType.Copy


def tile_attend_gdelta_kernel(tc, dyT, oT, wo_words, wo_scales, gq, offs, out_0, out_1):
    nc = tc.nc
    with ExitStack() as ctx:
        keep = ctx.enter_context(tc.tile_pool(name="keep", bufs=1))
        wide = ctx.enter_context(tc.tile_pool(name="wide", bufs=1))
        psum = ctx.enter_context(tc.psum_pool(name="psum", bufs=1))

        offsets = keep.tile([P, SLOTS // PER_COLUMN], U16, name="offsets")
        halves = [slice(h * HALF, (h + 1) * HALF) for h in range(2)]
        half_lists = [offsets[:, h * HALF // PER_COLUMN : (h + 1) * HALF // PER_COLUMN] for h in range(2)]

        w_scales = keep.tile([P, E], U8, name="w_scales", align_bytes=64)
        nc.gpsimd.memset(w_scales[:].bitcast(I32), 0)
        gate_table = keep.tile([P, T], F32, name="gate_table", tag="grouped0", align_bytes=64)
        nc.gpsimd.memset(gate_table[0 : P - 1, :].bitcast(I32), 0)
        nc.scalar.dma_start(out=gate_table[P - 1 : P, :], in_=gq[0:1, :])

        dy_rows = dyT.rearrange("(p t) w -> p t w", t=PACK)
        planes = [wide.tile([P, T], F32, name="dy%d" % t, offset=WORD_BYTES + ROW_BYTES * t) for t in range(PACK)]
        nc.sync.dma_start(out=planes[0][:], in_=dy_rows[:, 0, :])
        nc.sync.dma_start(offsets[:], offs)
        for t in range(1, PACK):
            nc.sync.dma_start(out=planes[t][:], in_=dy_rows[:, t, :])
        w_words = keep.tile([P, E], U32, name="w_words", align_bytes=64)
        nc.sync.dma_start(out=w_words[:].bitcast(I32), in_=wo_words[0].rearrange("p n t -> p (n t)").bitcast(I32))
        for quad in range(P // QUAD):
            nc.sync.dma_start(
                out=w_scales[QUAD * quad : QUAD * quad + 4, :].bitcast(I32),
                in_=wo_scales[0, 4 * quad : 4 * quad + 4, :].bitcast(I32),
            )

        ident = keep.tile([P, P], F32, name="ident")
        make_identity(nc, ident[:])
        delta_cols = keep.tile([P, QUAD], F32, name="delta_cols", align_bytes=64)
        nc.gpsimd.memset(delta_cols[:], 0.0)
        windows = {}
        for m in range(SLABS - 1):
            windows[m] = keep.tile([P, T], F32, name="window%d" % m)
            nc.gpsimd.memset(windows[m][:].bitcast(I32), 0)

        gate_row = keep.tile([P, SLOTS], F32, name="gate_row", tag="grouped1", align_bytes=64)
        nc.vector.tensor_copy(gate_row[:], gate_table[:].indirect(offsets[:]))
        gate_turned = psum.tile([P, BLOCKS, P], F32, name="gate_turned", tag="bank6")
        for j in range(BLOCKS):
            nc.tensor.transpose(gate_turned[:, j, :], gate_row[:, j * P : (j + 1) * P], ident[:])
        gate_cols = keep.tile([P, BLOCKS], F32, name="gate_cols")
        nc.scalar.activation(gate_cols[:], gate_turned[:, :, P - 1], COPY)
        gate_spread = psum.tile([P, BLOCKS, P], F32, name="gate_spread", tag="bank7")
        for j in range(BLOCKS):
            nc.tensor.transpose(gate_spread[:, j, :], gate_cols[:, j : j + 1].to_broadcast([P, P]), ident[:])
        gate = keep.tile([P, SLOTS], F32, name="gate")
        nc.scalar.copy(out=gate[:], in_=gate_spread[:].rearrange("p j s -> p (j s)"))

        grouped = [keep.tile([P, HALF, PACK], BF16, name="grouped%d" % h, tag="grouped%d" % h, align_bytes=64) for h in range(2)]
        for t in range(PACK):
            nc.vector.tensor_copy(grouped[0][:, :, t], planes[t][:].indirect(half_lists[0]))
            nc.scalar.activation(grouped[1][:, :, t], planes[t][:].indirect(half_lists[1]), COPY)

        dy_words = [
            wide.tile([P, HALF], U32, name="dy_words0", offset=ROW_BYTES * PACK, align_bytes=64),
            keep.tile([P, HALF], U32, name="dy_words1", align_bytes=64),
        ]
        dy_scales = [keep.tile([P, HALF], U8, name="dy_scales%d" % h, align_bytes=64) for h in range(2)]
        for h in (1, 0):
            nc.vector.quantize_mx(
                out=dy_words[h][:].bitcast(E5M2),
                scales=dy_scales[h][:],
                in_=grouped[h][:].rearrange("p s t -> p (s t)"),
            )

        o_rows = oT.rearrange("(m p) w -> p m w", p=P)
        o_pairs = [wide.tile([P, 2, T], F32, name="o_pair%d" % u, offset=2 * ROW_BYTES * u) for u in range(SLABS // 2)]
        for u in range(SLABS // 2):
            nc.sync.dma_start(out=o_pairs[u][:], in_=o_rows[:, 2 * u : 2 * u + 2, :])

        windows[3] = keep.tile([P, T], F32, name="window3", tag="grouped0", align_bytes=64)
        nc.gpsimd.memset(windows[3][:].bitcast(I32), 0)

        grads = [keep.tile([P, SLOTS], F32, name="grad%d" % m) for m in range(SLABS)]

        def product(m, h, out):
            nc.tensor.matmul_mx(
                out=out,
                lhsT=w_words[:, m * P : (m + 1) * P].bitcast(E4M3),
                lhsT_scale=w_scales[:, m * P : (m + 1) * P],
                rhs=dy_words[h][:].bitcast(E5M2),
                rhs_scale=dy_scales[h][:],
                start=True,
                stop=True,
            )

        def store(m):
            nc.sync.dma_start(out=out_0[m * P : (m + 1) * P, :], in_=windows[m][:])

        def banked_product(m, h, bank):
            prod = psum.tile([P, HALF], F32, name="prod", tag="bank%d" % bank)
            product(m, h, prod[:])
            return prod

        def gate_on_vector(m, h, bank):
            nc.vector.tensor_tensor(grads[m][:, halves[h]], banked_product(m, h, bank)[:], gate[:, halves[h]], MULT)

        def place_by_scalar(m, h):
            nc.scalar.activation(windows[m][:].indirect(half_lists[h]), grads[m][:, halves[h]], COPY)

        def place_by_vector(m, slots, entries):
            nc.vector.tensor_copy(windows[m][:].indirect(entries), grads[m][:, slots])

        for bank, (m, h) in enumerate([(0, 1), (1, 1), (1, 0)]):
            gate_on_vector(m, h, bank)
        place_by_scalar(0, 1)
        prod = psum.tile([P, SLOTS], F32, name="prod", tag="bank3")
        for h in (1, 0):
            product(2, h, prod[:, halves[h]])
        nc.vector.tensor_tensor(grads[2][:], prod[:], gate[:], MULT)
        gate_on_vector(3, 1, 0)
        ungated = keep.tile([P, HALF], F32, name="ungated")
        nc.scalar.copy(out=ungated[:], in_=banked_product(3, 0, 1)[:])
        nc.gpsimd.tensor_tensor(grads[3][:, halves[0]], ungated[:], gate[:, halves[0]], MULT)
        gate_on_vector(0, 0, 2)
        place_by_vector(2, halves[0], half_lists[0])
        place_by_scalar(0, 0)
        store(0)
        place_by_scalar(2, 1)
        store(2)
        for m in (1, 3):
            place_by_vector(m, slice(0, SLOTS), offsets[:])
            store(m)

        picks = [keep.tile([P, SLOTS], F32, name="pick%d" % m) for m in range(SLABS)]
        sums = [psum.tile([P, P], F32, name="sum%d" % j, tag="bank%d" % bank) for j, bank in enumerate((4, 5, 6, 7))]
        terms = [keep.tile([P, SLOTS], F32, name="term%d" % m) for m in range(SLABS)]
        last_pieces = [halves[0], slice(HALF, HALF + P), slice(HALF + P, SLOTS)]
        for m in range(SLABS):
            last = m == SLABS - 1
            for slots in last_pieces if last else halves:
                entries = offsets[:, slots.start // PER_COLUMN : slots.stop // PER_COLUMN]
                nc.scalar.activation(picks[m][:, slots], o_pairs[m // 2][:, m % 2, :].indirect(entries), COPY)
                engine = nc.vector if m * SLOTS + slots.start >= FIRST_ON_VECTOR else nc.gpsimd
                engine.tensor_tensor(terms[m][:, slots], picks[m][:, slots], grads[m][:, slots], MULT)
                for j in range(slots.start // P, slots.stop // P):
                    nc.tensor.matmul(
                        sums[j][:],
                        lhsT=terms[m][:, j * P : (j + 1) * P],
                        rhs=ident[:],
                        is_transpose=True,
                        start=m == 0,
                        stop=last,
                    )

        spent = keep.tile([P, 2, P], F32, name="spent")
        for j in range(BLOCKS):
            column = delta_cols[:, STEP * j : STEP * j + 1]
            if j in (0, BLOCKS - 1):
                nc.scalar.activation(spent[:, j % 2, :], sums[j][:], COPY, accum_out=column)
            else:
                nc.vector.tensor_reduce(out=column, in_=sums[j][:], op=ADD, axis=mybir.AxisListType.X)
        delta_rows = keep.tile([P, QUAD], F32, name="delta_rows", align_bytes=64)
        nc.vector.transpose(delta_rows[:], delta_cols[:])
        nc.scalar.dma_start(out=out_1[0].rearrange("(j q s) -> q j s", j=BLOCKS, q=P // QUAD), in_=delta_rows[0:P:STEP, :])
